import numpy as np
import ml_dtypes


def mxq(x, axis, fmt="e4m3"):
    dtype, down = {"e4m3": (ml_dtypes.float8_e4m3fn, 7), "e5m2": (ml_dtypes.float8_e5m2, 14)}[fmt]
    v = np.moveaxis(np.asarray(x, np.float32).astype(ml_dtypes.bfloat16).astype(np.float64), axis, -1)
    blocks = v.reshape(v.shape[:-1] + (-1, 32))
    amax = np.abs(blocks).max(-1, keepdims=True)
    byte = np.maximum(np.where(amax > 0, np.frexp(amax)[1] - 1 + 127, 0) - down, 1)
    scale = np.exp2(byte - 127.0)
    codes = (blocks / scale).astype(np.float32).astype(dtype).astype(np.float64)
    return np.moveaxis((codes * scale).reshape(v.shape), -1, axis)


WIDE = False


def mx_kscale(k):
    if not WIDE:
        return np.ones(k)
    levels = np.array([10, -10, 5, -5, 0])
    if k % 512:
        return np.exp2(np.random.permutation(np.resize(levels, k // 32))).repeat(32)
    a = np.empty((k // 512, 16))
    for p in range(k // 512):
        a[p, :8] = np.random.permutation(np.resize(levels, 8))
        for g in range(8):
            far = levels[np.abs(levels - a[p, g]) >= 10]
            a[p, g + 8] = far[np.random.randint(len(far))]
    return np.exp2(a.ravel()).repeat(32)


def f64(x):
    return np.asarray(x).astype(np.float64)


def striped(idx):
    return np.tile(np.asarray(idx).reshape(-1, 16).T, (8, 1)).astype(np.uint16)


def unstriped(offs):
    return offs[:16].T.reshape(-1).astype(np.int64)


E2M1 = np.array([0.0, 0.5, 1.0, 1.5, 2.0, 3.0, 4.0, 6.0, -0.0, -0.5, -1.0, -1.5, -2.0, -3.0, -4.0, -6.0])


def pack_weight(w, fmt):
    k, n = w.shape
    w = f64(np.asarray(w, np.float32).astype(ml_dtypes.bfloat16)).reshape(k // 32, 32, n)
    amax = np.abs(w).max(1)
    if fmt == "e4m3":
        byte = np.frexp(amax)[1] - 1 + 127 - 7
    else:
        mant, ex = np.frexp(amax / 6.0)
        byte = np.where(mant > 0.5, ex, ex - 1) + 127
    byte = np.clip(np.where(amax > 0, byte, 1), 1, 254)
    scaled = (w * np.exp2(127.0 - byte)[:, None, :]).reshape(k, n).astype(np.float32)
    by_word = np.ascontiguousarray(scaled.reshape(k // 512, 128, 4, n).transpose(0, 1, 3, 2))
    if fmt == "e4m3":
        words = by_word.astype(ml_dtypes.float8_e4m3fn).view(np.uint8)
    else:
        c = by_word.astype(ml_dtypes.float4_e2m1fn).view(np.uint8) & 0xF
        words = (c[..., 0::2] | (c[..., 1::2] << 4)).reshape(k // 512, 128, 2 * n)
    return np.ascontiguousarray(words), np.ascontiguousarray(byte.astype(np.uint8).reshape(k // 512, 16, n))


def unpack_weight(words, scales, fmt):
    g, _, n = scales.shape
    words = np.ascontiguousarray(words).reshape(g, 128, n, -1)
    if fmt == "e4m3":
        vals = words.view(ml_dtypes.float8_e4m3fn).astype(np.float64)
    else:
        nib = np.empty((g, 128, n, 4), np.uint8)
        nib[..., 0::2] = words & 0xF
        nib[..., 1::2] = words >> 4
        vals = E2M1[nib]
    vals = vals * np.repeat(np.exp2(scales.astype(np.float64) - 127.0), 8, axis=1)[..., None]
    return vals.transpose(0, 1, 3, 2).reshape(g * 512, n)


B, N, T, D, DV, NQ = 1, 512, 1024, 1024, 256, 256
CAP = 2.0


def setup_inputs():
    n = np.random.standard_normal
    idx = np.sort(np.random.permutation(T)[:B * N].reshape(B, N), axis=1).reshape(-1)
    s = mx_kscale(D)[:, None]
    u = np.ones(T)
    u[idx] = mx_kscale(B * N)
    r = np.random.uniform(0.5, 2.0, T)
    qp = [pack_weight(x, "e4m3") for x in n((B, D, NQ)) * s * (1.00 / np.sqrt(D))]
    k = n((D, T)) / s
    v = n((DV, T)) / (u * r)
    kp = pack_weight(k, "e2m1")
    return {
        "q_words": np.stack([x[0] for x in qp]),
        "q_scales": np.stack([x[1] for x in qp]),
        "k_words": np.ascontiguousarray(kp[0].reshape(D // 1024, 2, 128, T, 2).transpose(0, 2, 3, 1, 4)).reshape(D // 1024, 128, T, 4),
        "k_scales": kp[1],
        "vT": v.astype(np.float32),
        "vs": np.tile(u * r, (128, 1)).astype(np.float32),
        "kb": np.tile(n(T), (128, 1)).astype(np.float32),
        "offs": striped(idx),
    }


def reference(q_words, q_scales, k_words, k_scales, vT, vs, kb, offs):
    idx = unstriped(offs)
    k = unpack_weight(k_words.reshape(D // 1024, 128, T, 2, 2).transpose(0, 3, 1, 2, 4).reshape(D // 512, 128, 2 * T), k_scales, "e2m1")
    v = f64(vT)
    pick = lambda x: x[:, idx].reshape(x.shape[0], B, N).transpose(1, 0, 2)
    q = np.stack([unpack_weight(q_words[b], q_scales[b], "e4m3") for b in range(B)])
    score = q.transpose(0, 2, 1) @ pick(k)
    score = score + pick(f64(kb))[:, :1, :]
    score = CAP * np.tanh(score / CAP)
    m = score.max(-1, keepdims=True)
    p = np.exp(score - m)
    total = p.sum(-1, keepdims=True)
    w = p * pick(f64(vs))[:, :1, :]
    y = mxq(w, 2, "e4m3") @ mxq(pick(v).transpose(0, 2, 1), 1, "e4m3")
    y = y / total
    return y

@@ -1,0 +1,167 @@
+from contextlib import ExitStack
+
+import concourse.mybir as mybir
+from concourse.masks import make_identity
+
+N, T, D, DV, NQ = 512, 1024, 1024, 256, 256
+CAP = 2.0
+FLOPS = 2 * NQ * N * D + 2 * NQ * N * DV
+
+F32 = mybir.dt.float32
+BF16 = mybir.dt.bfloat16
+I32 = mybir.dt.int32
+U32 = mybir.dt.uint32
+U16 = mybir.dt.uint16
+U8 = mybir.dt.uint8
+FP8X4 = mybir.dt.float8_e4m3fn_x4
+FP4X4 = mybir.dt.float4_e2m1fn_x4
+ACT = mybir.ActivationFunctionType
+ALU = mybir.AluOpType
+
+P = 128
+PASSES = D // 512
+HALF = N // 2
+ROW = P - 1
+
+
+def tile_attend_soft_cap_kb_srtq256n512t1024_kernel(tc, q_words, q_scales, k_words, k_scales, vT, vs, kb, offs, out):
+    nc = tc.nc
+    with ExitStack() as ctx:
+        sb = ctx.enter_context(tc.tile_pool(name="sb", bufs=1))
+        ps = ctx.enter_context(tc.psum_pool(name="ps", bufs=1))
+
+        def bank(number, shape, name):
+            return ps.tile(shape, F32, name=name, tag="bank%d" % number)
+
+        offsets = sb.tile([P, N // 16], U16, name="offsets")
+        kb_pool = sb.tile([P, T], F32, name="kb_pool", tag="shared")
+        vs_pool = sb.tile([P, T], F32, name="vs_pool")
+        ks_pool = sb.tile([P, PASSES, T], U8, name="ks_pool", align_bytes=64)
+        kw_pool = sb.tile([P, T], U32, name="kw_pool", align_bytes=64)
+        q_codes = sb.tile([P, PASSES, NQ], U32, name="q_codes", align_bytes=64)
+        q_plane = sb.tile([P, PASSES, NQ], U8, name="q_plane", align_bytes=64)
+        v_low = sb.tile([P, T], F32, name="v_low")
+        ident = sb.tile([P, P], F32, name="ident")
+        warm = sb.tile([P, 1], F32, name="warm")
+        zero = sb.tile([P, 1], F32, name="zero")
+
+        nc.vector.memset(ks_pool[:].rearrange("p o t -> p (o t)").bitcast(I32), 0)
+        nc.vector.memset(q_plane[:].rearrange("p o t -> p (o t)").bitcast(I32), 0)
+        nc.vector.memset(zero[:], 0.0)
+        nc.scalar.activation(warm[:], zero[:], ACT.Exp)
+        nc.gpsimd.dma_start(v_low[:], vT[0:P, :])
+        nc.gpsimd.memset(kb_pool[0:ROW, :], 0.0)
+        make_identity(nc, ident[:])
+        nc.gpsimd.memset(vs_pool[0:ROW, :], 0.0)
+
+        nc.sync.dma_start(offsets[:], offs)
+        nc.sync.dma_start(kb_pool[ROW:P, :], kb[0:1, :])
+        nc.sync.dma_start(vs_pool[ROW:P, :], vs[0:1, :])
+        nc.sync.dma_start(kw_pool[:].bitcast(I32), k_words[0].rearrange("p t b -> p (t b)").bitcast(I32))
+        nc.sync.dma_start(q_codes[:].bitcast(I32), q_words[0].rearrange("o p q b -> p o (q b)").bitcast(I32))
+        for r in range(4):
+            nc.sync.dma_start(ks_pool[r:P:32, :, :].bitcast(I32),
+                              k_scales[:, r:16:4, :].rearrange("o f t -> f o t").bitcast(I32))
+        for r in range(4):
+            nc.sync.dma_start(q_plane[r:P:32, :, :].bitcast(I32),
+                              q_scales[0][:, r:16:4, :].rearrange("o f t -> f o t").bitcast(I32))
+
+        kb_listed = sb.tile([P, N], F32, name="kb_listed")
+        nc.vector.tensor_copy(kb_listed[:], kb_pool[:].indirect(offsets[:]))
+        v_high = sb.tile([P, T], F32, name="v_high", tag="shared")
+        nc.sync.dma_start(v_high[:], vT[P:2 * P, :])
+        kb_turned = bank(0, [P, 4, P], "kb_turned")
+        for j in range(4):
+            nc.tensor.transpose(kb_turned[:, j, :], kb_listed[:, j * P:(j + 1) * P], ident[:])
+        kb_half = sb.tile([P, 4], F32, name="kb_half")
+        nc.scalar.activation(kb_half[:], kb_turned[:, :, ROW], ACT.Copy, scale=1.0 / CAP)
+
+        turned = [bank(5 + qb, [P, N], "turned%d" % qb) for qb in range(2)]
+        v_listed = [sb.tile([P, 2, P, 2], BF16, name="v_listed%d" % h) for h in range(2)]
+        v_rounded = sb.tile([P, T], BF16, name="v_rounded")
+        nc.scalar.copy(v_rounded[:], v_low[:])
+        nc.scalar.activation(v_listed[0][:].rearrange("p u m r -> p m u r"), v_rounded[:].indirect(offsets[:]), ACT.Copy)
+
+        k_pairs = sb.tile([P, N], U32, name="k_pairs", align_bytes=64)
+        nc.vector.tensor_copy(k_pairs[:], kw_pool[:].indirect(offsets[:]))
+        k_codes = sb.tile([P, PASSES, N], U16, name="k_codes", align_bytes=64)
+        nc.vector.tensor_copy(k_codes[:], k_pairs[:].bitcast(U16).rearrange("p (n o) -> p o n", o=PASSES))
+        capped = []
+        for first, count in ((0, 1), (1, 1), (2, 2)):
+            piece = offsets[:, first * 8:(first + count) * 8]
+            k_plane = sb.tile([P, PASSES, count * P], U8, name="k_plane%d" % first, align_bytes=64)
+            for o in range(PASSES):
+                nc.vector.tensor_copy(k_plane[:, o, :], ks_pool[:, o, :].indirect(piece))
+            for jj in range(count):
+                j = first + jj
+                scores = bank(1 + j, [P, NQ], "scores%d" % j)
+                for qb in range(2):
+                    rows = slice(qb * P, (qb + 1) * P)
+                    for o in range(PASSES):
+                        nc.tensor.matmul_mx(
+                            out=scores[:, rows],
+                            lhsT=k_codes[:, o, j * P:(j + 1) * P].bitcast(FP4X4),
+                            lhsT_scale=k_plane[:, o, jj * P:(jj + 1) * P],
+                            rhs=q_codes[:, o, rows].bitcast(FP8X4), rhs_scale=q_plane[:, o, rows],
+                            start=(o == 0), stop=(o == PASSES - 1))
+                tanh = sb.tile([P, NQ], F32, name="tanh%d" % j)
+                nc.scalar.activation(tanh[:], scores[:], ACT.Tanh, bias=kb_half[:, j:j + 1], scale=1.0 / CAP)
+                capped.append(tanh)
+        for j in range(4):
+            for qb in range(2):
+                nc.tensor.transpose(turned[qb][:, j * P:(j + 1) * P], capped[j][:, qb * P:(qb + 1) * P], ident[:])
+
+        vs_listed = sb.tile([P, N], F32, name="vs_listed")
+        nc.vector.tensor_copy(vs_listed[:], vs_pool[:].indirect(offsets[:]))
+        nc.vector.tensor_copy(v_listed[1][:].rearrange("p u m r -> p m u r"), v_high[:].indirect(offsets[:]))
+
+        probs, total = [], []
+        for qb in range(2):
+            neg_c = sb.tile([P, 4, P], F32, name="neg_c%d" % qb)
+            neg_m = sb.tile([P, 1], F32, name="neg_m%d" % qb)
+            nc.vector.tensor_scalar(out=neg_c[:], in0=turned[qb][:].rearrange("q (m t) -> q t m", t=4),
+                                    scalar1=-CAP, scalar2=None, op0=ALU.mult, op1=ALU.min, accum_out=neg_m[:])
+            p = sb.tile([P, N], F32, name="p%d" % qb)
+            l = sb.tile([P, 1], F32, name="l%d" % qb)
+            nc.scalar.activation(p[:], neg_c[:].rearrange("q t m -> q (t m)"), ACT.Exp,
+                                 bias=neg_m[:], scale=-1.0, accum_out=l[:])
+            probs.append(p)
+            total.append(l)
+
+        vs_turned = bank(7, [P, 4, P], "vs_turned")
+        for t in range(4):
+            nc.tensor.transpose(vs_turned[:, t, :], vs_listed[:, t:N:4], ident[:])
+        vs_col = sb.tile([P, 4], F32, name="vs_col")
+        nc.scalar.copy(vs_col[:], vs_turned[:, :, ROW])
+
+        v_turned = bank(0, [P, 2, 2, P], "v_turned")
+        for h in range(2):
+            words = v_listed[h][:].rearrange("p u m r -> p (u m r)").bitcast(F32)
+            for u in range(2):
+                nc.tensor.transpose(v_turned[:, h, u, :], words[:, u * P:(u + 1) * P], ident[:])
+        v_grouped = sb.tile([P, DV * 4], BF16, name="v_grouped", align_bytes=64)
+        nc.scalar.copy(v_grouped[:].bitcast(F32).rearrange("p (h e u) -> p h e u", h=2, u=2),
+                       v_turned[:].rearrange("p h u e -> p h e u"))
+        v_codes = sb.tile([P, DV], U32, name="v_codes", align_bytes=64)
+        v_plane = sb.tile([P, DV], U8, name="v_plane", align_bytes=64)
+        nc.vector.quantize_mx(out=v_codes[:].bitcast(FP8X4), scales=v_plane[:], in_=v_grouped[:])
+
+        for qb in range(2):
+            p_turned = bank(1 + qb, [P, 4, P], "p_turned%d" % qb)
+            for t in range(4):
+                nc.tensor.transpose(p_turned[:, t, :], probs[qb][:, t * P:(t + 1) * P], ident[:])
+            w = sb.tile([P, P, 4], BF16, name="w%d" % qb, align_bytes=64)
+            nc.vector.tensor_tensor(w[:], p_turned[:].rearrange("p t q -> p q t"),
+                                    vs_col[:].unsqueeze(1).to_broadcast([P, P, 4]), ALU.mult)
+            inverse = sb.tile([P, 1], F32, name="inverse%d" % qb)
+            nc.vector.reciprocal(inverse[:], total[qb][:])
+            w_codes = sb.tile([P, P], U32, name="w_codes%d" % qb, align_bytes=64)
+            w_plane = sb.tile([P, P], U8, name="w_plane%d" % qb, align_bytes=64)
+            nc.vector.quantize_mx(out=w_codes[:].bitcast(FP8X4), scales=w_plane[:],
+                                  in_=w[:].rearrange("p q t -> p (q t)"))
+            sums = bank(3 + qb, [P, DV], "sums%d" % qb)
+            nc.tensor.matmul_mx(out=sums[:], lhsT=w_codes[:].bitcast(FP8X4), lhsT_scale=w_plane[:],
+                                rhs=v_codes[:].bitcast(FP8X4), rhs_scale=v_plane[:], start=True, stop=True)
+            y = sb.tile([P, DV], F32, name="y%d" % qb)
+            nc.scalar.activation(y[:], sums[:], ACT.Copy, scale=inverse[:])
+            nc.sync.dma_start(out[0, qb * P:(qb + 1) * P, :], y[:])

@@ -1,7 +1,6 @@
 from contextlib import ExitStack
 
 import concourse.mybir as mybir
-from concourse.masks import make_identity
 
 N, T, D, DV, NQ = 512, 1024, 1024, 256, 256
 CAP = 2.0
@@ -19,8 +18,8 @@ ACT = mybir.ActivationFunctionType
 ALU = mybir.AluOpType
 
 P = 128
+QUAD = 32
 PASSES = D // 512
-HALF = N // 2
 ROW = P - 1
 
 
@@ -30,138 +29,156 @@ def tile_attend_soft_cap_kb_srtq256n512t1024_kernel(tc, q_words, q_scales, k_wor
         sb = ctx.enter_context(tc.tile_pool(name="sb", bufs=1))
         ps = ctx.enter_context(tc.psum_pool(name="ps", bufs=1))
 
+        def tile(shape, dtype, name, tag=None):
+            return sb.tile(shape, dtype, name=name, tag=tag or name, align_bytes=64)
+
         def bank(number, shape, name):
             return ps.tile(shape, F32, name=name, tag="bank%d" % number)
 
         offsets = sb.tile([P, N // 16], U16, name="offsets")
-        kb_pool = sb.tile([P, T], F32, name="kb_pool", tag="shared")
-        vs_pool = sb.tile([P, T], F32, name="vs_pool")
-        ks_pool = sb.tile([P, PASSES, T], U8, name="ks_pool", align_bytes=64)
-        kw_pool = sb.tile([P, T], U32, name="kw_pool", align_bytes=64)
-        q_codes = sb.tile([P, PASSES, NQ], U32, name="q_codes", align_bytes=64)
-        q_plane = sb.tile([P, PASSES, NQ], U8, name="q_plane", align_bytes=64)
-        v_low = sb.tile([P, T], F32, name="v_low")
-        ident = sb.tile([P, P], F32, name="ident")
-        warm = sb.tile([P, 1], F32, name="warm")
-        zero = sb.tile([P, 1], F32, name="zero")
+        ks_pool = tile([P, T], U8, "ks_pool", "ks_then_values")
+        kb_pool = tile([P, T], F32, "kb_pool", "kb_then_scales")
+        ks_second = tile([P, N], U8, "ks_second")
+        v_low = tile([P, T], F32, "v_low")
 
-        nc.vector.memset(ks_pool[:].rearrange("p o t -> p (o t)").bitcast(I32), 0)
-        nc.vector.memset(q_plane[:].rearrange("p o t -> p (o t)").bitcast(I32), 0)
-        nc.vector.memset(zero[:], 0.0)
-        nc.scalar.activation(warm[:], zero[:], ACT.Exp)
-        nc.gpsimd.dma_start(v_low[:], vT[0:P, :])
+        nc.gpsimd.memset(ks_pool[:].bitcast(I32), 0)
         nc.gpsimd.memset(kb_pool[0:ROW, :], 0.0)
-        make_identity(nc, ident[:])
-        nc.gpsimd.memset(vs_pool[0:ROW, :], 0.0)
-
+        nc.gpsimd.memset(ks_second[3 * QUAD:P, :].bitcast(I32), 0)
         nc.sync.dma_start(offsets[:], offs)
         nc.sync.dma_start(kb_pool[ROW:P, :], kb[0:1, :])
-        nc.sync.dma_start(vs_pool[ROW:P, :], vs[0:1, :])
-        nc.sync.dma_start(kw_pool[:].bitcast(I32), k_words[0].rearrange("p t b -> p (t b)").bitcast(I32))
-        nc.sync.dma_start(q_codes[:].bitcast(I32), q_words[0].rearrange("o p q b -> p o (q b)").bitcast(I32))
-        for r in range(4):
-            nc.sync.dma_start(ks_pool[r:P:32, :, :].bitcast(I32),
-                              k_scales[:, r:16:4, :].rearrange("o f t -> f o t").bitcast(I32))
-        for r in range(4):
-            nc.sync.dma_start(q_plane[r:P:32, :, :].bitcast(I32),
-                              q_scales[0][:, r:16:4, :].rearrange("o f t -> f o t").bitcast(I32))
+        nc.sync.dma_start(v_low[:], vT[0:P, :])
+        for g in range(P // QUAD):
+            queue = (nc.scalar, nc.sync)[g // 2]
+            queue.dma_start(ks_pool[g * QUAD:g * QUAD + 8, :].bitcast(I32),
+                            k_scales[:, 4 * g:4 * g + 4, :].bitcast(I32))
 
-        kb_listed = sb.tile([P, N], F32, name="kb_listed")
+        ones = tile([P, P], F32, "ones", "ones_then_keys")
+        quad_start = tile([P, 1], F32, "quad_start")
+        nc.vector.memset(ones[:], 1.0)
+        column = tile([P, P], F32, "column", "column_then_queries")
+        nc.vector.tensor_tensor_scan(column[:], ones[:], ones[:], -1.0, ALU.mult, ALU.add)
+        for g in range(P // QUAD):
+            nc.vector.memset(quad_start[g * QUAD:(g + 1) * QUAD, :], float(g * QUAD))
+        in_quad = tile([P, QUAD], F32, "in_quad", "in_quad_then_plane")
+        nc.vector.transpose(in_quad[:], column[:, 0:QUAD])
+        ident = tile([P, P], F32, "ident")
+        nc.vector.tensor_scalar(out=ident[:], in0=column[:], scalar1=quad_start[:], scalar2=in_quad[:, 0:1],
+                                op0=ALU.subtract, op1=ALU.is_equal)
+        warm = tile([P, 1], F32, "warm", "warm_then_vs")
+        nc.scalar.activation(warm[:], ident[:, 0:1], ACT.Exp)
+
+        kw_pool = tile([P, T], U32, "kw_pool", "ones_then_keys")
+        nc.sync.dma_start(kw_pool[:].bitcast(I32), k_words[0].rearrange("p t b -> p (t b)").bitcast(I32))
+        q_codes = tile([P, PASSES, NQ], U32, "q_codes", "column_then_queries")
+        nc.sync.dma_start(q_codes[:].bitcast(I32), q_words[0].rearrange("o p q b -> p o (q b)").bitcast(I32))
+        q_plane = tile([P, PASSES, NQ], U8, "q_plane", "in_quad_then_plane")
+        nc.vector.memset(q_plane[:].rearrange("p o t -> p (o t)").bitcast(I32), 0)
+        for r in range(4):
+            nc.sync.dma_start(q_plane[r:P:QUAD, :, :].bitcast(I32),
+                              q_scales[0][:, r:16:4, :].rearrange("o f t -> f o t").bitcast(I32))
+        vs_pool = tile([P, T], F32, "vs_pool", "warm_then_vs")
+        nc.sync.dma_start(vs_pool[:], vs)
+
+        kb_listed = tile([P, N], F32, "kb_listed")
         nc.vector.tensor_copy(kb_listed[:], kb_pool[:].indirect(offsets[:]))
-        v_high = sb.tile([P, T], F32, name="v_high", tag="shared")
-        nc.sync.dma_start(v_high[:], vT[P:2 * P, :])
         kb_turned = bank(0, [P, 4, P], "kb_turned")
         for j in range(4):
             nc.tensor.transpose(kb_turned[:, j, :], kb_listed[:, j * P:(j + 1) * P], ident[:])
-        kb_half = sb.tile([P, 4], F32, name="kb_half")
-        nc.scalar.activation(kb_half[:], kb_turned[:, :, ROW], ACT.Copy, scale=1.0 / CAP)
 
-        turned = [bank(5 + qb, [P, N], "turned%d" % qb) for qb in range(2)]
-        v_listed = [sb.tile([P, 2, P, 2], BF16, name="v_listed%d" % h) for h in range(2)]
-        v_rounded = sb.tile([P, T], BF16, name="v_rounded")
+        ks_listed = tile([P, N], U8, "ks_listed", "kb_then_scales")
+        nc.vector.tensor_copy(ks_listed[:], ks_pool[:].indirect(offsets[:]))
+        for first, count in ((0, 64), (64, 32), (96, 4)):
+            nc.sync.dma_start(ks_second[first:first + count, :].bitcast(I32),
+                              ks_listed[first + 4:first + 4 + count, :].bitcast(I32))
+        planes = (ks_listed, ks_second)
+        v_high = tile([P, T], F32, "v_high", "ks_then_values")
+        nc.sync.dma_start(v_high[:], vT[P:2 * P, :])
+
+        v_rounded = tile([P, T], BF16, "v_rounded")
         nc.scalar.copy(v_rounded[:], v_low[:])
-        nc.scalar.activation(v_listed[0][:].rearrange("p u m r -> p m u r"), v_rounded[:].indirect(offsets[:]), ACT.Copy)
+        kb_half = tile([P, 4], F32, "kb_half")
+        nc.scalar.activation(kb_half[:], kb_turned[:, :, ROW], ACT.Copy, scale=1.0 / CAP)
+        v_listed_low = tile([P, N], BF16, "v_listed_low")
+        nc.scalar.activation(v_listed_low[:], v_rounded[:].indirect(offsets[:]), ACT.Copy)
 
-        k_pairs = sb.tile([P, N], U32, name="k_pairs", align_bytes=64)
-        nc.vector.tensor_copy(k_pairs[:], kw_pool[:].indirect(offsets[:]))
-        k_codes = sb.tile([P, PASSES, N], U16, name="k_codes", align_bytes=64)
-        nc.vector.tensor_copy(k_codes[:], k_pairs[:].bitcast(U16).rearrange("p (n o) -> p o n", o=PASSES))
-        capped = []
-        for first, count in ((0, 1), (1, 1), (2, 2)):
-            piece = offsets[:, first * 8:(first + count) * 8]
-            k_plane = sb.tile([P, PASSES, count * P], U8, name="k_plane%d" % first, align_bytes=64)
-            for o in range(PASSES):
-                nc.vector.tensor_copy(k_plane[:, o, :], ks_pool[:, o, :].indirect(piece))
-            for jj in range(count):
-                j = first + jj
-                scores = bank(1 + j, [P, NQ], "scores%d" % j)
-                for qb in range(2):
+        capped = {}
+        for j in range(4):
+            slots = slice(j * P, (j + 1) * P)
+            pairs = tile([P, P], U32, "k_pairs%d" % j)
+            nc.vector.tensor_copy(pairs[:], kw_pool[:].indirect(offsets[:, j * 8:(j + 1) * 8]))
+            codes = tile([P, PASSES, P], U16, "k_codes%d" % j)
+            nc.vector.tensor_copy(codes[:], pairs[:].bitcast(U16).rearrange("p (n o) -> p o n", o=PASSES))
+            for blocks, number in (((0, 1), 1 + j),) if j < 3 else (((0,), 4), ((1,), 7)):
+                scores = bank(number, [P, len(blocks), P], "scores%d_%d" % (j, blocks[0]))
+                for at, qb in enumerate(blocks):
                     rows = slice(qb * P, (qb + 1) * P)
                     for o in range(PASSES):
                         nc.tensor.matmul_mx(
-                            out=scores[:, rows],
-                            lhsT=k_codes[:, o, j * P:(j + 1) * P].bitcast(FP4X4),
-                            lhsT_scale=k_plane[:, o, jj * P:(jj + 1) * P],
+                            out=scores[:, at, :], lhsT=codes[:, o, :].bitcast(FP4X4), lhsT_scale=planes[o][:, slots],
                             rhs=q_codes[:, o, rows].bitcast(FP8X4), rhs_scale=q_plane[:, o, rows],
                             start=(o == 0), stop=(o == PASSES - 1))
-                tanh = sb.tile([P, NQ], F32, name="tanh%d" % j)
+                tanh = tile([P, len(blocks), P], F32, "tanh%d_%d" % (j, blocks[0]))
                 nc.scalar.activation(tanh[:], scores[:], ACT.Tanh, bias=kb_half[:, j:j + 1], scale=1.0 / CAP)
-                capped.append(tanh)
-        for j in range(4):
-            for qb in range(2):
-                nc.tensor.transpose(turned[qb][:, j * P:(j + 1) * P], capped[j][:, qb * P:(qb + 1) * P], ident[:])
-
-        vs_listed = sb.tile([P, N], F32, name="vs_listed")
-        nc.vector.tensor_copy(vs_listed[:], vs_pool[:].indirect(offsets[:]))
-        nc.vector.tensor_copy(v_listed[1][:].rearrange("p u m r -> p m u r"), v_high[:].indirect(offsets[:]))
-
-        probs, total = [], []
+                for at, qb in enumerate(blocks):
+                    capped[j, qb] = tanh[:, at, :]
+        turned = [bank(5 - qb, [P, N], "turned%d" % qb) for qb in range(2)]
         for qb in range(2):
-            neg_c = sb.tile([P, 4, P], F32, name="neg_c%d" % qb)
-            neg_m = sb.tile([P, 1], F32, name="neg_m%d" % qb)
-            nc.vector.tensor_scalar(out=neg_c[:], in0=turned[qb][:].rearrange("q (m t) -> q t m", t=4),
-                                    scalar1=-CAP, scalar2=None, op0=ALU.mult, op1=ALU.min, accum_out=neg_m[:])
-            p = sb.tile([P, N], F32, name="p%d" % qb)
-            l = sb.tile([P, 1], F32, name="l%d" % qb)
-            nc.scalar.activation(p[:], neg_c[:].rearrange("q t m -> q (t m)"), ACT.Exp,
-                                 bias=neg_m[:], scale=-1.0, accum_out=l[:])
-            probs.append(p)
+            for j in range(4):
+                nc.tensor.transpose(turned[qb][:, j * P:(j + 1) * P], capped[j, qb], ident[:])
+
+        vs_listed = tile([P, N], F32, "vs_listed", "k_pairs3")
+        nc.vector.tensor_copy(vs_listed[:], vs_pool[:].indirect(offsets[:]))
+        v_listed_high = tile([P, N], BF16, "v_listed_high", "warm_then_vs")
+        nc.vector.tensor_copy(v_listed_high[:], v_high[:].indirect(offsets[:]))
+
+        neg_m = []
+        neg_c = tile([P, 2, N], F32, "neg_c", "ks_then_values")
+        for qb in range(2):
+            m = tile([P, 1], F32, "neg_m%d" % qb)
+            nc.vector.tensor_scalar(out=neg_c[:, qb, :], in0=turned[qb][:], scalar1=-CAP, scalar2=None,
+                                    op0=ALU.mult, op1=ALU.min, accum_out=m[:])
+            neg_m.append(m)
+
+        v_turned = bank(7, [P, 2, 2, P], "v_turned")
+        for h, listed in enumerate((v_listed_low, v_listed_high)):
+            words = listed[:].bitcast(F32)
+            for u in range(2):
+                nc.tensor.transpose(v_turned[:, h, u, :], words[:, u:2 * P:2], ident[:])
+
+        weights, total = [], []
+        for qb in range(2):
+            p = tile([P, 2, P, 2], F32, "p%d" % qb)
+            l = tile([P, 1], F32, "l%d" % qb)
+            nc.scalar.activation(p[:], turned[qb][:].rearrange("q (m u r) -> q u m r", u=2, r=2), ACT.Exp,
+                                 bias=neg_m[qb][:], scale=CAP, accum_out=l[:])
+            w = tile([P, 2, P, 2], BF16, "w%d" % qb)
+            nc.vector.tensor_tensor(w[:], p[:], vs_listed[:].rearrange("q (m u r) -> q u m r", u=2, r=2), ALU.mult)
+            weights.append(w)
             total.append(l)
 
-        vs_turned = bank(7, [P, 4, P], "vs_turned")
-        for t in range(4):
-            nc.tensor.transpose(vs_turned[:, t, :], vs_listed[:, t:N:4], ident[:])
-        vs_col = sb.tile([P, 4], F32, name="vs_col")
-        nc.scalar.copy(vs_col[:], vs_turned[:, :, ROW])
-
-        v_turned = bank(0, [P, 2, 2, P], "v_turned")
-        for h in range(2):
-            words = v_listed[h][:].rearrange("p u m r -> p (u m r)").bitcast(F32)
-            for u in range(2):
-                nc.tensor.transpose(v_turned[:, h, u, :], words[:, u * P:(u + 1) * P], ident[:])
-        v_grouped = sb.tile([P, DV * 4], BF16, name="v_grouped", align_bytes=64)
+        v_grouped = tile([P, DV * 4], BF16, "v_grouped", "neg_m1")
         nc.scalar.copy(v_grouped[:].bitcast(F32).rearrange("p (h e u) -> p h e u", h=2, u=2),
                        v_turned[:].rearrange("p h u e -> p h e u"))
-        v_codes = sb.tile([P, DV], U32, name="v_codes", align_bytes=64)
-        v_plane = sb.tile([P, DV], U8, name="v_plane", align_bytes=64)
+        v_codes = tile([P, DV], U32, "v_codes")
+        v_plane = tile([P, DV], U8, "v_plane")
         nc.vector.quantize_mx(out=v_codes[:].bitcast(FP8X4), scales=v_plane[:], in_=v_grouped[:])
 
         for qb in range(2):
-            p_turned = bank(1 + qb, [P, 4, P], "p_turned%d" % qb)
-            for t in range(4):
-                nc.tensor.transpose(p_turned[:, t, :], probs[qb][:, t * P:(t + 1) * P], ident[:])
-            w = sb.tile([P, P, 4], BF16, name="w%d" % qb, align_bytes=64)
-            nc.vector.tensor_tensor(w[:], p_turned[:].rearrange("p t q -> p q t"),
-                                    vs_col[:].unsqueeze(1).to_broadcast([P, P, 4]), ALU.mult)
-            inverse = sb.tile([P, 1], F32, name="inverse%d" % qb)
+            w_turned = bank(1 + qb, [P, 2, P], "w_turned%d" % qb)
+            words = weights[qb][:].rearrange("q u m r -> q u (m r)").bitcast(F32)
+            for u in range(2):
+                nc.tensor.transpose(w_turned[:, u, :], words[:, u, :], ident[:])
+            w_grouped = tile([P, P * 4], BF16, "w_grouped%d" % qb)
+            nc.scalar.copy(w_grouped[:].bitcast(F32).rearrange("p (q u) -> p q u", u=2),
+                           w_turned[:].rearrange("p u q -> p q u"))
+            w_codes = tile([P, P], U32, "w_codes%d" % qb)
+            w_plane = tile([P, P], U8, "w_plane%d" % qb)
+            nc.vector.quantize_mx(out=w_codes[:].bitcast(FP8X4), scales=w_plane[:], in_=w_grouped[:])
+            inverse = tile([P, 1], F32, "inverse%d" % qb)
             nc.vector.reciprocal(inverse[:], total[qb][:])
-            w_codes = sb.tile([P, P], U32, name="w_codes%d" % qb, align_bytes=64)
-            w_plane = sb.tile([P, P], U8, name="w_plane%d" % qb, align_bytes=64)
-            nc.vector.quantize_mx(out=w_codes[:].bitcast(FP8X4), scales=w_plane[:],
-                                  in_=w[:].rearrange("p q t -> p (q t)"))
-            sums = bank(3 + qb, [P, DV], "sums%d" % qb)
+            sums = bank(3 * (1 - qb), [P, DV], "sums%d" % qb)
             nc.tensor.matmul_mx(out=sums[:], lhsT=w_codes[:].bitcast(FP8X4), lhsT_scale=w_plane[:],
                                 rhs=v_codes[:].bitcast(FP8X4), rhs_scale=v_plane[:], start=True, stop=True)
-            y = sb.tile([P, DV], F32, name="y%d" % qb)
+            y = tile([P, DV], F32, "y%d" % qb)
             nc.scalar.activation(y[:], sums[:], ACT.Copy, scale=inverse[:])
             nc.sync.dma_start(out[0, qb * P:(qb + 1) * P, :], y[:])

@@ -101,34 +101,40 @@ def tile_attend_soft_cap_kb_srtq256n512t1024_kernel(tc, q_words, q_scales, k_wor
         v_listed_low = tile([P, N], BF16, "v_listed_low")
         nc.scalar.activation(v_listed_low[:], v_rounded[:].indirect(offsets[:]), ACT.Copy)
 
-        capped = {}
-        for j in range(4):
-            slots = slice(j * P, (j + 1) * P)
-            pairs = tile([P, P], U32, "k_pairs%d" % j)
-            nc.vector.tensor_copy(pairs[:], kw_pool[:].indirect(offsets[:, j * 8:(j + 1) * 8]))
-            codes = tile([P, PASSES, P], U16, "k_codes%d" % j)
+        k_codes, scores = [], {}
+        for h in range(2):
+            pairs = tile([P, 2 * P], U32, "k_pairs%d" % h)
+            nc.vector.tensor_copy(pairs[:], kw_pool[:].indirect(offsets[:, h * 16:(h + 1) * 16]))
+            codes = tile([P, PASSES, 2 * P], U16, "k_codes%d" % h)
             nc.vector.tensor_copy(codes[:], pairs[:].bitcast(U16).rearrange("p (n o) -> p o n", o=PASSES))
-            for blocks, number in (((0, 1), 1 + j),) if j < 3 else (((0,), 4), ((1,), 7)):
-                scores = bank(number, [P, len(blocks), P], "scores%d_%d" % (j, blocks[0]))
-                for at, qb in enumerate(blocks):
-                    rows = slice(qb * P, (qb + 1) * P)
-                    for o in range(PASSES):
-                        nc.tensor.matmul_mx(
-                            out=scores[:, at, :], lhsT=codes[:, o, :].bitcast(FP4X4), lhsT_scale=planes[o][:, slots],
-                            rhs=q_codes[:, o, rows].bitcast(FP8X4), rhs_scale=q_plane[:, o, rows],
-                            start=(o == 0), stop=(o == PASSES - 1))
-                tanh = tile([P, len(blocks), P], F32, "tanh%d_%d" % (j, blocks[0]))
-                nc.scalar.activation(tanh[:], scores[:], ACT.Tanh, bias=kb_half[:, j:j + 1], scale=1.0 / CAP)
-                for at, qb in enumerate(blocks):
-                    capped[j, qb] = tanh[:, at, :]
-        turned = [bank(5 - qb, [P, N], "turned%d" % qb) for qb in range(2)]
+            k_codes.extend([codes[:, :, 0:P], codes[:, :, P:2 * P]])
+
+        def score_pass(j, qb, o):
+            rows = slice(qb * P, (qb + 1) * P)
+            nc.tensor.matmul_mx(
+                out=scores[j, qb][:], lhsT=k_codes[j][:, o, :].bitcast(FP4X4),
+                lhsT_scale=planes[o][:, j * P:(j + 1) * P],
+                rhs=q_codes[:, o, rows].bitcast(FP8X4), rhs_scale=q_plane[:, o, rows],
+                start=(o == 0), stop=(o == PASSES - 1))
+
+        capped = {}
         for qb in range(2):
             for j in range(4):
-                nc.tensor.transpose(turned[qb][:, j * P:(j + 1) * P], capped[j, qb], ident[:])
+                scores[j, qb] = bank(7 - 2 * j - qb, [P, P], "scores%d_%d" % (j, qb))
+                score_pass(j, qb, 0)
+            for j in range(4):
+                score_pass(j, qb, 1)
+                capped[j, qb] = tile([P, P], F32, "tanh%d_%d" % (j, qb))
+                nc.scalar.activation(capped[j, qb][:], scores[j, qb][:], ACT.Tanh,
+                                     bias=kb_half[:, j:j + 1], scale=1.0 / CAP)
+        turned = [bank((7, 1)[qb], [P, N], "turned%d" % qb) for qb in range(2)]
+        for qb in range(2):
+            for j in range(4):
+                nc.tensor.transpose(turned[qb][:, j * P:(j + 1) * P], capped[j, qb][:], ident[:])
 
-        vs_listed = tile([P, N], F32, "vs_listed", "k_pairs3")
+        vs_listed = tile([P, N], F32, "vs_listed", "k_pairs0")
         nc.vector.tensor_copy(vs_listed[:], vs_pool[:].indirect(offsets[:]))
-        v_listed_high = tile([P, N], BF16, "v_listed_high", "warm_then_vs")
+        v_listed_high = tile([P, N], BF16, "v_listed_high", "k_pairs1")
         nc.vector.tensor_copy(v_listed_high[:], v_high[:].indirect(offsets[:]))
 
         neg_m = []
@@ -139,7 +145,7 @@ def tile_attend_soft_cap_kb_srtq256n512t1024_kernel(tc, q_words, q_scales, k_wor
                                     op0=ALU.mult, op1=ALU.min, accum_out=m[:])
             neg_m.append(m)
 
-        v_turned = bank(7, [P, 2, 2, P], "v_turned")
+        v_turned = bank(0, [P, 2, 2, P], "v_turned")
         for h, listed in enumerate((v_listed_low, v_listed_high)):
             words = listed[:].bitcast(F32)
             for u in range(2):
@@ -164,7 +170,7 @@ def tile_attend_soft_cap_kb_srtq256n512t1024_kernel(tc, q_words, q_scales, k_wor
         nc.vector.quantize_mx(out=v_codes[:].bitcast(FP8X4), scales=v_plane[:], in_=v_grouped[:])
 
         for qb in range(2):
-            w_turned = bank(1 + qb, [P, 2, P], "w_turned%d" % qb)
+            w_turned = bank(2 + qb, [P, 2, P], "w_turned%d" % qb)
             words = weights[qb][:].rearrange("q u m r -> q u (m r)").bitcast(F32)
             for u in range(2):
                 nc.tensor.transpose(w_turned[:, u, :], words[:, u, :], ident[:])
@@ -176,7 +182,7 @@ def tile_attend_soft_cap_kb_srtq256n512t1024_kernel(tc, q_words, q_scales, k_wor
             nc.vector.quantize_mx(out=w_codes[:].bitcast(FP8X4), scales=w_plane[:], in_=w_grouped[:])
             inverse = tile([P, 1], F32, "inverse%d" % qb)
             nc.vector.reciprocal(inverse[:], total[qb][:])
-            sums = bank(3 * (1 - qb), [P, DV], "sums%d" % qb)
+            sums = bank(4 + qb, [P, DV], "sums%d" % qb)
             nc.tensor.matmul_mx(out=sums[:], lhsT=w_codes[:].bitcast(FP8X4), lhsT_scale=w_plane[:],
                                 rhs=v_codes[:].bitcast(FP8X4), rhs_scale=v_plane[:], start=True, stop=True)
             y = tile([P, DV], F32, "y%d" % qb)

@@ -43,17 +43,17 @@ def tile_attend_soft_cap_kb_srtq256n512t1024_kernel(tc, q_words, q_scales, k_wor
 
         nc.gpsimd.memset(ks_pool[:].bitcast(I32), 0)
         nc.gpsimd.memset(kb_pool[0:ROW, :], 0.0)
-        nc.gpsimd.memset(ks_second[3 * QUAD:P, :].bitcast(I32), 0)
         nc.sync.dma_start(offsets[:], offs)
         nc.sync.dma_start(kb_pool[ROW:P, :], kb[0:1, :])
         nc.sync.dma_start(v_low[:], vT[0:P, :])
-        for g in range(P // QUAD):
-            queue = (nc.scalar, nc.sync)[g // 2]
-            queue.dma_start(ks_pool[g * QUAD:g * QUAD + 8, :].bitcast(I32),
-                            k_scales[:, 4 * g:4 * g + 4, :].bitcast(I32))
+        groups = k_scales.rearrange("o (g r) t -> (o g) r t", r=4).bitcast(I32)
+        for g in range(2):
+            nc.scalar.dma_start(ks_pool[g * QUAD:g * QUAD + 16, :].bitcast(I32), groups[g:8:2])
+        for g in range(2, 4):
+            nc.sync.dma_start(ks_pool[g * QUAD:g * QUAD + 4, :].bitcast(I32), groups[g])
 
         ones = tile([P, P], F32, "ones", "ones_then_keys")
-        quad_start = tile([P, 1], F32, "quad_start")
+        quad_start = tile([P, 1], F32, "quad_start", "quad_then_vs")
         nc.vector.memset(ones[:], 1.0)
         column = tile([P, P], F32, "column", "column_then_queries")
         nc.vector.tensor_tensor_scan(column[:], ones[:], ones[:], -1.0, ALU.mult, ALU.add)
@@ -64,7 +64,7 @@ def tile_attend_soft_cap_kb_srtq256n512t1024_kernel(tc, q_words, q_scales, k_wor
         ident = tile([P, P], F32, "ident")
         nc.vector.tensor_scalar(out=ident[:], in0=column[:], scalar1=quad_start[:], scalar2=in_quad[:, 0:1],
                                 op0=ALU.subtract, op1=ALU.is_equal)
-        warm = tile([P, 1], F32, "warm", "warm_then_vs")
+        warm = tile([P, 1], F32, "warm")
         nc.scalar.activation(warm[:], ident[:, 0:1], ACT.Exp)
 
         kw_pool = tile([P, T], U32, "kw_pool", "ones_then_keys")
@@ -73,11 +73,11 @@ def tile_attend_soft_cap_kb_srtq256n512t1024_kernel(tc, q_words, q_scales, k_wor
         nc.sync.dma_start(q_codes[:].bitcast(I32), q_words[0].rearrange("o p q b -> p o (q b)").bitcast(I32))
         q_plane = tile([P, PASSES, NQ], U8, "q_plane", "in_quad_then_plane")
         nc.vector.memset(q_plane[:].rearrange("p o t -> p (o t)").bitcast(I32), 0)
+        vs_pool = tile([P, T], F32, "vs_pool", "quad_then_vs")
+        nc.sync.dma_start(vs_pool[:], vs)
         for r in range(4):
             nc.sync.dma_start(q_plane[r:P:QUAD, :, :].bitcast(I32),
                               q_scales[0][:, r:16:4, :].rearrange("o f t -> f o t").bitcast(I32))
-        vs_pool = tile([P, T], F32, "vs_pool", "warm_then_vs")
-        nc.sync.dma_start(vs_pool[:], vs)
 
         kb_listed = tile([P, N], F32, "kb_listed")
         nc.vector.tensor_copy(kb_listed[:], kb_pool[:].indirect(offsets[:]))
@@ -87,16 +87,16 @@ def tile_attend_soft_cap_kb_srtq256n512t1024_kernel(tc, q_words, q_scales, k_wor
 
         ks_listed = tile([P, N], U8, "ks_listed", "kb_then_scales")
         nc.vector.tensor_copy(ks_listed[:], ks_pool[:].indirect(offsets[:]))
-        for first, count in ((0, 64), (64, 32), (96, 4)):
-            nc.sync.dma_start(ks_second[first:first + count, :].bitcast(I32),
-                              ks_listed[first + 4:first + 4 + count, :].bitcast(I32))
+        for half, source in enumerate((8, 12)):
+            nc.sync.dma_start(ks_second[half * 64:(half + 1) * 64, :].bitcast(I32),
+                              ks_listed[source:source + 64, :].bitcast(I32))
         planes = (ks_listed, ks_second)
         v_high = tile([P, T], F32, "v_high", "ks_then_values")
         nc.sync.dma_start(v_high[:], vT[P:2 * P, :])
 
         v_rounded = tile([P, T], BF16, "v_rounded")
         nc.scalar.copy(v_rounded[:], v_low[:])
-        kb_half = tile([P, 4], F32, "kb_half")
+        kb_half = tile([P, 4], F32, "kb_half", "v_low")
         nc.scalar.activation(kb_half[:], kb_turned[:, :, ROW], ACT.Copy, scale=1.0 / CAP)
         v_listed_low = tile([P, N], BF16, "v_listed_low")
         nc.scalar.activation(v_listed_low[:], v_rounded[:].indirect(offsets[:]), ACT.Copy)
@@ -158,7 +158,9 @@ def tile_attend_soft_cap_kb_srtq256n512t1024_kernel(tc, q_words, q_scales, k_wor
             nc.scalar.activation(p[:], turned[qb][:].rearrange("q (m u r) -> q u m r", u=2, r=2), ACT.Exp,
                                  bias=neg_m[qb][:], scale=CAP, accum_out=l[:])
             w = tile([P, 2, P, 2], BF16, "w%d" % qb)
-            nc.vector.tensor_tensor(w[:], p[:], vs_listed[:].rearrange("q (m u r) -> q u m r", u=2, r=2), ALU.mult)
+            for u in range(2):
+                nc.vector.tensor_tensor(w[:, u], p[:, u], vs_listed[:].rearrange("q (m u r) -> q u m r", u=2, r=2)[:, u],
+                                        ALU.mult)
             weights.append(w)
             total.append(l)
 
@@ -182,9 +184,16 @@ def tile_attend_soft_cap_kb_srtq256n512t1024_kernel(tc, q_words, q_scales, k_wor
             nc.vector.quantize_mx(out=w_codes[:].bitcast(FP8X4), scales=w_plane[:], in_=w_grouped[:])
             inverse = tile([P, 1], F32, "inverse%d" % qb)
             nc.vector.reciprocal(inverse[:], total[qb][:])
-            sums = bank(4 + qb, [P, DV], "sums%d" % qb)
-            nc.tensor.matmul_mx(out=sums[:], lhsT=w_codes[:].bitcast(FP8X4), lhsT_scale=w_plane[:],
-                                rhs=v_codes[:].bitcast(FP8X4), rhs_scale=v_plane[:], start=True, stop=True)
             y = tile([P, DV], F32, "y%d" % qb)
-            nc.scalar.activation(y[:], sums[:], ACT.Copy, scale=inverse[:])
+            width = DV // (qb + 1)
+            for h in range(qb + 1):
+                cols = slice(h * width, (h + 1) * width)
+                sums = bank(4 + qb + h, [P, width], "sums%d_%d" % (qb, h))
+                nc.tensor.matmul_mx(out=sums[:], lhsT=w_codes[:].bitcast(FP8X4), lhsT_scale=w_plane[:],
+                                    rhs=v_codes[:, cols].bitcast(FP8X4), rhs_scale=v_plane[:, cols],
+                                    start=True, stop=True)
+                if h == 0:
+                    nc.scalar.activation(y[:, cols], sums[:], ACT.Copy, scale=inverse[:])
+                else:
+                    nc.vector.tensor_scalar(out=y[:, cols], in0=sums[:], scalar1=inverse[:], scalar2=None, op0=ALU.mult)
             nc.sync.dma_start(out[0, qb * P:(qb + 1) * P, :], y[:])

@@ -53,7 +53,7 @@ def tile_attend_soft_cap_kb_srtq256n512t1024_kernel(tc, q_words, q_scales, k_wor
             nc.sync.dma_start(ks_pool[g * QUAD:g * QUAD + 4, :].bitcast(I32), groups[g])
 
         ones = tile([P, P], F32, "ones", "ones_then_keys")
-        quad_start = tile([P, 1], F32, "quad_start", "quad_then_vs")
+        quad_start = tile([P, 1], F32, "quad_start")
         nc.vector.memset(ones[:], 1.0)
         column = tile([P, P], F32, "column", "column_then_queries")
         nc.vector.tensor_tensor_scan(column[:], ones[:], ones[:], -1.0, ALU.mult, ALU.add)
@@ -64,7 +64,7 @@ def tile_attend_soft_cap_kb_srtq256n512t1024_kernel(tc, q_words, q_scales, k_wor
         ident = tile([P, P], F32, "ident")
         nc.vector.tensor_scalar(out=ident[:], in0=column[:], scalar1=quad_start[:], scalar2=in_quad[:, 0:1],
                                 op0=ALU.subtract, op1=ALU.is_equal)
-        warm = tile([P, 1], F32, "warm")
+        warm = tile([P, 1], F32, "warm", "warm_then_vs")
         nc.scalar.activation(warm[:], ident[:, 0:1], ACT.Exp)
 
         kw_pool = tile([P, T], U32, "kw_pool", "ones_then_keys")
@@ -73,11 +73,11 @@ def tile_attend_soft_cap_kb_srtq256n512t1024_kernel(tc, q_words, q_scales, k_wor
         nc.sync.dma_start(q_codes[:].bitcast(I32), q_words[0].rearrange("o p q b -> p o (q b)").bitcast(I32))
         q_plane = tile([P, PASSES, NQ], U8, "q_plane", "in_quad_then_plane")
         nc.vector.memset(q_plane[:].rearrange("p o t -> p (o t)").bitcast(I32), 0)
-        vs_pool = tile([P, T], F32, "vs_pool", "quad_then_vs")
-        nc.sync.dma_start(vs_pool[:], vs)
         for r in range(4):
             nc.sync.dma_start(q_plane[r:P:QUAD, :, :].bitcast(I32),
                               q_scales[0][:, r:16:4, :].rearrange("o f t -> f o t").bitcast(I32))
+        vs_pool = tile([P, T], F32, "vs_pool", "warm_then_vs")
+        nc.sync.dma_start(vs_pool[:], vs)
 
         kb_listed = tile([P, N], F32, "kb_listed")
         nc.vector.tensor_copy(kb_listed[:], kb_pool[:].indirect(offsets[:]))

@@ -39,23 +39,21 @@ def tile_attend_soft_cap_kb_srtq256n512t1024_kernel(tc, q_words, q_scales, k_wor
         ks_pool = tile([P, T], U8, "ks_pool", "ks_then_values")
         kb_pool = tile([P, T], F32, "kb_pool", "kb_then_scales")
         ks_second = tile([P, N], U8, "ks_second")
-        v_low = tile([P, T], F32, "v_low")
+        ones = tile([P, P], F32, "ones", "ones_then_keys")
 
+        nc.gpsimd.memset(ones[:], 1.0)
         nc.gpsimd.memset(ks_pool[:].bitcast(I32), 0)
         nc.gpsimd.memset(kb_pool[0:ROW, :], 0.0)
         nc.sync.dma_start(offsets[:], offs)
         nc.sync.dma_start(kb_pool[ROW:P, :], kb[0:1, :])
-        nc.sync.dma_start(v_low[:], vT[0:P, :])
         groups = k_scales.rearrange("o (g r) t -> (o g) r t", r=4).bitcast(I32)
         for g in range(2):
             nc.scalar.dma_start(ks_pool[g * QUAD:g * QUAD + 16, :].bitcast(I32), groups[g:8:2])
         for g in range(2, 4):
             nc.sync.dma_start(ks_pool[g * QUAD:g * QUAD + 4, :].bitcast(I32), groups[g])
 
-        ones = tile([P, P], F32, "ones", "ones_then_keys")
-        quad_start = tile([P, 1], F32, "quad_start")
-        nc.vector.memset(ones[:], 1.0)
-        column = tile([P, P], F32, "column", "column_then_queries")
+        quad_start = tile([P, 1], F32, "quad_start", "quad_then_queries")
+        column = tile([P, P], F32, "column", "column_then_values")
         nc.vector.tensor_tensor_scan(column[:], ones[:], ones[:], -1.0, ALU.mult, ALU.add)
         for g in range(P // QUAD):
             nc.vector.memset(quad_start[g * QUAD:(g + 1) * QUAD, :], float(g * QUAD))
@@ -69,7 +67,9 @@ def tile_attend_soft_cap_kb_srtq256n512t1024_kernel(tc, q_words, q_scales, k_wor
 
         kw_pool = tile([P, T], U32, "kw_pool", "ones_then_keys")
         nc.sync.dma_start(kw_pool[:].bitcast(I32), k_words[0].rearrange("p t b -> p (t b)").bitcast(I32))
-        q_codes = tile([P, PASSES, NQ], U32, "q_codes", "column_then_queries")
+        v_low = tile([P, T], F32, "v_low", "column_then_values")
+        nc.sync.dma_start(v_low[:], vT[0:P, :])
+        q_codes = tile([P, PASSES, NQ], U32, "q_codes", "quad_then_queries")
         nc.sync.dma_start(q_codes[:].bitcast(I32), q_words[0].rearrange("o p q b -> p o (q b)").bitcast(I32))
         q_plane = tile([P, PASSES, NQ], U8, "q_plane", "in_quad_then_plane")
         nc.vector.memset(q_plane[:].rearrange("p o t -> p (o t)").bitcast(I32), 0)
@@ -96,7 +96,7 @@ def tile_attend_soft_cap_kb_srtq256n512t1024_kernel(tc, q_words, q_scales, k_wor
 
         v_rounded = tile([P, T], BF16, "v_rounded")
         nc.scalar.copy(v_rounded[:], v_low[:])
-        kb_half = tile([P, 4], F32, "kb_half", "v_low")
+        kb_half = tile([P, 4], F32, "kb_half", "column_then_values")
         nc.scalar.activation(kb_half[:], kb_turned[:, :, ROW], ACT.Copy, scale=1.0 / CAP)
         v_listed_low = tile([P, N], BF16, "v_listed_low")
         nc.scalar.activation(v_listed_low[:], v_rounded[:].indirect(offsets[:]), ACT.Copy)

@@ -102,12 +102,26 @@ def tile_attend_soft_cap_kb_srtq256n512t1024_kernel(tc, q_words, q_scales, k_wor
         nc.scalar.activation(v_listed_low[:], v_rounded[:].indirect(offsets[:]), ACT.Copy)
 
         k_codes, scores = [], {}
-        for h in range(2):
-            pairs = tile([P, 2 * P], U32, "k_pairs%d" % h)
-            nc.vector.tensor_copy(pairs[:], kw_pool[:].indirect(offsets[:, h * 16:(h + 1) * 16]))
-            codes = tile([P, PASSES, 2 * P], U16, "k_codes%d" % h)
-            nc.vector.tensor_copy(codes[:], pairs[:].bitcast(U16).rearrange("p (n o) -> p o n", o=PASSES))
-            k_codes.extend([codes[:, :, 0:P], codes[:, :, P:2 * P]])
+        pieces = ((0, 2), (2, 1), (3, 1))
+        k_pairs = []
+
+        def gather_words(h):
+            first, count = pieces[h]
+            pairs = tile([P, count * P], U32, "k_pairs%d" % h)
+            nc.vector.tensor_copy(pairs[:], kw_pool[:].indirect(offsets[:, first * 8:(first + count) * 8]))
+            k_pairs.append(pairs)
+
+        def part_words(h):
+            count = pieces[h][1]
+            codes = tile([P, PASSES, count * P], U16, "k_codes%d" % h)
+            nc.vector.tensor_copy(codes[:], k_pairs[h][:].bitcast(U16).rearrange("p (n o) -> p o n", o=PASSES))
+            k_codes.extend(codes[:, :, j * P:(j + 1) * P] for j in range(count))
+
+        gather_words(0)
+        for h in range(len(pieces)):
+            if h + 1 < len(pieces):
+                gather_words(h + 1)
+            part_words(h)
 
         def score_pass(j, qb, o):
             rows = slice(qb * P, (qb + 1) * P)
@@ -117,11 +131,12 @@ def tile_attend_soft_cap_kb_srtq256n512t1024_kernel(tc, q_words, q_scales, k_wor
                 rhs=q_codes[:, o, rows].bitcast(FP8X4), rhs_scale=q_plane[:, o, rows],
                 start=(o == 0), stop=(o == PASSES - 1))
 
-        capped = {}
-        for qb in range(2):
-            for j in range(4):
+        for j in range(4):
+            for qb in range(2):
                 scores[j, qb] = bank(7 - 2 * j - qb, [P, P], "scores%d_%d" % (j, qb))
                 score_pass(j, qb, 0)
+        capped = {}
+        for qb in range(2):
             for j in range(4):
                 score_pass(j, qb, 1)
                 capped[j, qb] = tile([P, P], F32, "tanh%d_%d" % (j, qb))
@@ -132,9 +147,9 @@ def tile_attend_soft_cap_kb_srtq256n512t1024_kernel(tc, q_words, q_scales, k_wor
             for j in range(4):
                 nc.tensor.transpose(turned[qb][:, j * P:(j + 1) * P], capped[j, qb][:], ident[:])
 
-        vs_listed = tile([P, N], F32, "vs_listed", "k_pairs0")
+        vs_listed = tile([P, N], F32, "vs_listed", "k_pairs1")
         nc.vector.tensor_copy(vs_listed[:], vs_pool[:].indirect(offsets[:]))
-        v_listed_high = tile([P, N], BF16, "v_listed_high", "k_pairs1")
+        v_listed_high = tile([P, N], BF16, "v_listed_high", "k_pairs2")
         nc.vector.tensor_copy(v_listed_high[:], v_high[:].indirect(offsets[:]))
 
         neg_m = []

@@ -39,13 +39,15 @@ def tile_attend_soft_cap_kb_srtq256n512t1024_kernel(tc, q_words, q_scales, k_wor
         ks_pool = tile([P, T], U8, "ks_pool", "ks_then_values")
         kb_pool = tile([P, T], F32, "kb_pool", "kb_then_scales")
         ks_second = tile([P, N], U8, "ks_second")
-        ones = tile([P, P], F32, "ones", "ones_then_keys")
+        ones = tile([P, P], F32, "ones", "ones_then_values")
 
         nc.gpsimd.memset(ones[:], 1.0)
         nc.gpsimd.memset(ks_pool[:].bitcast(I32), 0)
         nc.gpsimd.memset(kb_pool[0:ROW, :], 0.0)
         nc.sync.dma_start(offsets[:], offs)
         nc.sync.dma_start(kb_pool[ROW:P, :], kb[0:1, :])
+        kw_pool = tile([P, T], U32, "kw_pool")
+        nc.sync.dma_start(kw_pool[:].bitcast(I32), k_words[0].rearrange("p t b -> p (t b)").bitcast(I32))
         groups = k_scales.rearrange("o (g r) t -> (o g) r t", r=4).bitcast(I32)
         for g in range(2):
             nc.scalar.dma_start(ks_pool[g * QUAD:g * QUAD + 16, :].bitcast(I32), groups[g:8:2])
@@ -53,7 +55,7 @@ def tile_attend_soft_cap_kb_srtq256n512t1024_kernel(tc, q_words, q_scales, k_wor
             nc.sync.dma_start(ks_pool[g * QUAD:g * QUAD + 4, :].bitcast(I32), groups[g])
 
         quad_start = tile([P, 1], F32, "quad_start", "quad_then_queries")
-        column = tile([P, P], F32, "column", "column_then_values")
+        column = tile([P, P], F32, "column")
         nc.vector.tensor_tensor_scan(column[:], ones[:], ones[:], -1.0, ALU.mult, ALU.add)
         for g in range(P // QUAD):
             nc.vector.memset(quad_start[g * QUAD:(g + 1) * QUAD, :], float(g * QUAD))
@@ -65,9 +67,7 @@ def tile_attend_soft_cap_kb_srtq256n512t1024_kernel(tc, q_words, q_scales, k_wor
         warm = tile([P, 1], F32, "warm", "warm_then_vs")
         nc.scalar.activation(warm[:], ident[:, 0:1], ACT.Exp)
 
-        kw_pool = tile([P, T], U32, "kw_pool", "ones_then_keys")
-        nc.sync.dma_start(kw_pool[:].bitcast(I32), k_words[0].rearrange("p t b -> p (t b)").bitcast(I32))
-        v_low = tile([P, T], F32, "v_low", "column_then_values")
+        v_low = tile([P, T], F32, "v_low", "ones_then_values")
         nc.sync.dma_start(v_low[:], vT[0:P, :])
         q_codes = tile([P, PASSES, NQ], U32, "q_codes", "quad_then_queries")
         nc.sync.dma_start(q_codes[:].bitcast(I32), q_words[0].rearrange("o p q b -> p o (q b)").bitcast(I32))
@@ -96,7 +96,7 @@ def tile_attend_soft_cap_kb_srtq256n512t1024_kernel(tc, q_words, q_scales, k_wor
 
         v_rounded = tile([P, T], BF16, "v_rounded")
         nc.scalar.copy(v_rounded[:], v_low[:])
-        kb_half = tile([P, 4], F32, "kb_half", "column_then_values")
+        kb_half = tile([P, 4], F32, "kb_half", "ones_then_values")
         nc.scalar.activation(kb_half[:], kb_turned[:, :, ROW], ACT.Copy, scale=1.0 / CAP)
         v_listed_low = tile([P, N], BF16, "v_listed_low")
         nc.scalar.activation(v_listed_low[:], v_rounded[:].indirect(offsets[:]), ACT.Copy)

@@ -36,7 +36,7 @@ def tile_attend_soft_cap_kb_srtq256n512t1024_kernel(tc, q_words, q_scales, k_wor
             return ps.tile(shape, F32, name=name, tag="bank%d" % number)
 
         offsets = sb.tile([P, N // 16], U16, name="offsets")
-        ks_pool = tile([P, T], U8, "ks_pool", "ks_then_values")
+        ks_pool = tile([P, T], U8, "ks_pool", "ks_then_words")
         kb_pool = tile([P, T], F32, "kb_pool", "kb_then_scales")
         ks_second = tile([P, N], U8, "ks_second")
         ones = tile([P, P], F32, "ones", "ones_then_values")
@@ -79,7 +79,7 @@ def tile_attend_soft_cap_kb_srtq256n512t1024_kernel(tc, q_words, q_scales, k_wor
         vs_pool = tile([P, T], F32, "vs_pool", "warm_then_vs")
         nc.sync.dma_start(vs_pool[:], vs)
 
-        kb_listed = tile([P, N], F32, "kb_listed")
+        kb_listed = tile([P, N], F32, "kb_listed", "kb_then_values")
         nc.vector.tensor_copy(kb_listed[:], kb_pool[:].indirect(offsets[:]))
         kb_turned = bank(0, [P, 4, P], "kb_turned")
         for j in range(4):
@@ -91,7 +91,7 @@ def tile_attend_soft_cap_kb_srtq256n512t1024_kernel(tc, q_words, q_scales, k_wor
             nc.sync.dma_start(ks_second[half * 64:(half + 1) * 64, :].bitcast(I32),
                               ks_listed[source:source + 64, :].bitcast(I32))
         planes = (ks_listed, ks_second)
-        v_high = tile([P, T], F32, "v_high", "ks_then_values")
+        v_high = tile([P, T], F32, "v_high", "kb_then_values")
         nc.sync.dma_start(v_high[:], vT[P:2 * P, :])
 
         v_rounded = tile([P, T], BF16, "v_rounded")
@@ -103,18 +103,18 @@ def tile_attend_soft_cap_kb_srtq256n512t1024_kernel(tc, q_words, q_scales, k_wor
 
         k_codes, scores = [], {}
         pieces = ((0, 2), (2, 1), (3, 1))
-        k_pairs = []
+        k_pairs = tile([P, N], U32, "k_pairs", "ks_then_words")
 
         def gather_words(h):
             first, count = pieces[h]
-            pairs = tile([P, count * P], U32, "k_pairs%d" % h)
-            nc.vector.tensor_copy(pairs[:], kw_pool[:].indirect(offsets[:, first * 8:(first + count) * 8]))
-            k_pairs.append(pairs)
+            nc.vector.tensor_copy(k_pairs[:, first * P:(first + count) * P],
+                                  kw_pool[:].indirect(offsets[:, first * 8:(first + count) * 8]))
 
         def part_words(h):
-            count = pieces[h][1]
+            first, count = pieces[h]
+            pairs = k_pairs[:, first * P:(first + count) * P]
             codes = tile([P, PASSES, count * P], U16, "k_codes%d" % h)
-            nc.vector.tensor_copy(codes[:], k_pairs[h][:].bitcast(U16).rearrange("p (n o) -> p o n", o=PASSES))
+            nc.vector.tensor_copy(codes[:], pairs.bitcast(U16).rearrange("p (n o) -> p o n", o=PASSES))
             k_codes.extend(codes[:, :, j * P:(j + 1) * P] for j in range(count))
 
         gather_words(0)
@@ -147,13 +147,13 @@ def tile_attend_soft_cap_kb_srtq256n512t1024_kernel(tc, q_words, q_scales, k_wor
             for j in range(4):
                 nc.tensor.transpose(turned[qb][:, j * P:(j + 1) * P], capped[j, qb][:], ident[:])
 
-        vs_listed = tile([P, N], F32, "vs_listed", "k_pairs1")
+        vs_listed = tile([P, N], F32, "vs_listed", "ks_then_words")
         nc.vector.tensor_copy(vs_listed[:], vs_pool[:].indirect(offsets[:]))
-        v_listed_high = tile([P, N], BF16, "v_listed_high", "k_pairs2")
+        v_listed_high = tile([P, N], BF16, "v_listed_high", "warm_then_vs")
         nc.vector.tensor_copy(v_listed_high[:], v_high[:].indirect(offsets[:]))
 
         neg_m = []
-        neg_c = tile([P, 2, N], F32, "neg_c", "ks_then_values")
+        neg_c = tile([P, 2, N], F32, "neg_c", "kb_then_values")
         for qb in range(2):
             m = tile([P, 1], F32, "neg_m%d" % qb)
             nc.vector.tensor_scalar(out=neg_c[:, qb, :], in0=turned[qb][:], scalar1=-CAP, scalar2=None,

@@ -101,32 +101,19 @@ def tile_attend_soft_cap_kb_srtq256n512t1024_kernel(tc, q_words, q_scales, k_wor
         v_listed_low = tile([P, N], BF16, "v_listed_low")
         nc.scalar.activation(v_listed_low[:], v_rounded[:].indirect(offsets[:]), ACT.Copy)
 
-        k_codes, scores = [], {}
-        pieces = ((0, 2), (2, 1), (3, 1))
-        k_pairs = tile([P, N], U32, "k_pairs", "ks_then_words")
-
-        def gather_words(h):
-            first, count = pieces[h]
-            nc.vector.tensor_copy(k_pairs[:, first * P:(first + count) * P],
-                                  kw_pool[:].indirect(offsets[:, first * 8:(first + count) * 8]))
-
-        def part_words(h):
-            first, count = pieces[h]
-            pairs = k_pairs[:, first * P:(first + count) * P]
-            codes = tile([P, PASSES, count * P], U16, "k_codes%d" % h)
-            nc.vector.tensor_copy(codes[:], pairs.bitcast(U16).rearrange("p (n o) -> p o n", o=PASSES))
-            k_codes.extend(codes[:, :, j * P:(j + 1) * P] for j in range(count))
-
-        gather_words(0)
-        for h in range(len(pieces)):
-            if h + 1 < len(pieces):
-                gather_words(h + 1)
-            part_words(h)
+        scores = {}
+        k_pairs = tile([P, N], U32, "k_pairs")
+        nc.vector.tensor_copy(k_pairs[:], kw_pool[:].indirect(offsets[:]))
+        k_codes = tile([P, PASSES, N], U16, "k_codes", "ks_then_words")
+        for h in range(2):
+            slots = slice(h * N // 2, (h + 1) * N // 2)
+            nc.vector.tensor_copy(k_codes[:, :, slots],
+                                  k_pairs[:, slots].bitcast(U16).rearrange("p (n o) -> p o n", o=PASSES))
 
         def score_pass(j, qb, o):
             rows = slice(qb * P, (qb + 1) * P)
             nc.tensor.matmul_mx(
-                out=scores[j, qb][:], lhsT=k_codes[j][:, o, :].bitcast(FP4X4),
+                out=scores[j, qb][:], lhsT=k_codes[:, o, j * P:(j + 1) * P].bitcast(FP4X4),
                 lhsT_scale=planes[o][:, j * P:(j + 1) * P],
                 rhs=q_codes[:, o, rows].bitcast(FP8X4), rhs_scale=q_plane[:, o, rows],
                 start=(o == 0), stop=(o == PASSES - 1))
@@ -147,9 +134,9 @@ def tile_attend_soft_cap_kb_srtq256n512t1024_kernel(tc, q_words, q_scales, k_wor
             for j in range(4):
                 nc.tensor.transpose(turned[qb][:, j * P:(j + 1) * P], capped[j, qb][:], ident[:])
 
-        vs_listed = tile([P, N], F32, "vs_listed", "ks_then_words")
+        vs_listed = tile([P, N], F32, "vs_listed")
         nc.vector.tensor_copy(vs_listed[:], vs_pool[:].indirect(offsets[:]))
-        v_listed_high = tile([P, N], BF16, "v_listed_high", "warm_then_vs")
+        v_listed_high = tile([P, N], BF16, "v_listed_high")
         nc.vector.tensor_copy(v_listed_high[:], v_high[:].indirect(offsets[:]))
 
         neg_m = []

@@ -136,8 +136,10 @@ def tile_attend_soft_cap_kb_srtq256n512t1024_kernel(tc, q_words, q_scales, k_wor
 
         vs_listed = tile([P, N], F32, "vs_listed")
         nc.vector.tensor_copy(vs_listed[:], vs_pool[:].indirect(offsets[:]))
-        v_listed_high = tile([P, N], BF16, "v_listed_high")
-        nc.vector.tensor_copy(v_listed_high[:], v_high[:].indirect(offsets[:]))
+        v_rounded_high = tile([P, T], BF16, "v_rounded_high")
+        nc.vector.tensor_copy(v_rounded_high[:], v_high[:])
+        v_listed_high = tile([P, N], BF16, "v_listed_high", "ones_then_values")
+        nc.scalar.activation(v_listed_high[:], v_rounded_high[:].indirect(offsets[:]), ACT.Copy)
 
         neg_m = []
         neg_c = tile([P, 2, N], F32, "neg_c", "kb_then_values")

@@ -149,11 +149,11 @@ def tile_attend_soft_cap_kb_srtq256n512t1024_kernel(tc, q_words, q_scales, k_wor
                                     op0=ALU.mult, op1=ALU.min, accum_out=m[:])
             neg_m.append(m)
 
-        v_turned = bank(0, [P, 2, 2, P], "v_turned")
+        v_turned = bank(0, [P, 2, P, 2], "v_turned")
         for h, listed in enumerate((v_listed_low, v_listed_high)):
             words = listed[:].bitcast(F32)
             for u in range(2):
-                nc.tensor.transpose(v_turned[:, h, u, :], words[:, u:2 * P:2], ident[:])
+                nc.tensor.transpose(v_turned[:, h, :, u], words[:, u:2 * P:2], ident[:])
 
         weights, total = [], []
         for qb in range(2):
@@ -169,20 +169,18 @@ def tile_attend_soft_cap_kb_srtq256n512t1024_kernel(tc, q_words, q_scales, k_wor
             total.append(l)
 
         v_grouped = tile([P, DV * 4], BF16, "v_grouped", "neg_m1")
-        nc.scalar.copy(v_grouped[:].bitcast(F32).rearrange("p (h e u) -> p h e u", h=2, u=2),
-                       v_turned[:].rearrange("p h u e -> p h e u"))
+        nc.scalar.copy(v_grouped[:].bitcast(F32), v_turned[:].rearrange("p h e u -> p (h e u)"))
         v_codes = tile([P, DV], U32, "v_codes")
         v_plane = tile([P, DV], U8, "v_plane")
         nc.vector.quantize_mx(out=v_codes[:].bitcast(FP8X4), scales=v_plane[:], in_=v_grouped[:])
 
         for qb in range(2):
-            w_turned = bank(2 + qb, [P, 2, P], "w_turned%d" % qb)
+            w_turned = bank(2 + qb, [P, P, 2], "w_turned%d" % qb)
             words = weights[qb][:].rearrange("q u m r -> q u (m r)").bitcast(F32)
             for u in range(2):
-                nc.tensor.transpose(w_turned[:, u, :], words[:, u, :], ident[:])
+                nc.tensor.transpose(w_turned[:, :, u], words[:, u, :], ident[:])
             w_grouped = tile([P, P * 4], BF16, "w_grouped%d" % qb)
-            nc.scalar.copy(w_grouped[:].bitcast(F32).rearrange("p (q u) -> p q u", u=2),
-                           w_turned[:].rearrange("p u q -> p q u"))
+            nc.scalar.copy(w_grouped[:].bitcast(F32), w_turned[:].rearrange("p q u -> p (q u)"))
             w_codes = tile([P, P], U32, "w_codes%d" % qb)
             w_plane = tile([P, P], U8, "w_plane%d" % qb)
             nc.vector.quantize_mx(out=w_codes[:].bitcast(FP8X4), scales=w_plane[:], in_=w_grouped[:])

@@ -132,7 +132,8 @@ def tile_attend_soft_cap_kb_srtq256n512t1024_kernel(tc, q_words, q_scales, k_wor
         turned = [bank((7, 1)[qb], [P, N], "turned%d" % qb) for qb in range(2)]
         for qb in range(2):
             for j in range(4):
-                nc.tensor.transpose(turned[qb][:, j * P:(j + 1) * P], capped[j, qb][:], ident[:])
+                dealt = turned[qb][:].rearrange("q (u m r) -> q m u r", u=2, r=2)
+                nc.tensor.transpose(dealt[:, j * QUAD:(j + 1) * QUAD], capped[j, qb][:], ident[:])
 
         vs_listed = tile([P, N], F32, "vs_listed")
         nc.vector.tensor_copy(vs_listed[:], vs_pool[:].indirect(offsets[:]))
@@ -159,7 +160,7 @@ def tile_attend_soft_cap_kb_srtq256n512t1024_kernel(tc, q_words, q_scales, k_wor
         for qb in range(2):
             p = tile([P, 2, P, 2], F32, "p%d" % qb)
             l = tile([P, 1], F32, "l%d" % qb)
-            nc.scalar.activation(p[:], turned[qb][:].rearrange("q (m u r) -> q u m r", u=2, r=2), ACT.Exp,
+            nc.scalar.activation(p[:], turned[qb][:].rearrange("q (u m r) -> q u m r", u=2, r=2), ACT.Exp,
                                  bias=neg_m[qb][:], scale=CAP, accum_out=l[:])
             w = tile([P, 2, P, 2], BF16, "w%d" % qb)
             for u in range(2):

@@ -37,46 +37,42 @@ def tile_attend_soft_cap_kb_srtq256n512t1024_kernel(tc, q_words, q_scales, k_wor
 
         offsets = sb.tile([P, N // 16], U16, name="offsets")
         ks_pool = tile([P, T], U8, "ks_pool", "ks_then_words")
-        kb_pool = tile([P, T], F32, "kb_pool", "kb_then_scales")
-        ks_second = tile([P, N], U8, "ks_second")
-        ones = tile([P, P], F32, "ones", "ones_then_values")
-
-        nc.gpsimd.memset(ones[:], 1.0)
-        nc.gpsimd.memset(ks_pool[:].bitcast(I32), 0)
-        nc.gpsimd.memset(kb_pool[0:ROW, :], 0.0)
+        nc.vector.memset(ks_pool[:].bitcast(I32), 0)
         nc.sync.dma_start(offsets[:], offs)
+        kb_pool = tile([P, T], F32, "kb_pool", "kb_then_scales")
         nc.sync.dma_start(kb_pool[ROW:P, :], kb[0:1, :])
         kw_pool = tile([P, T], U32, "kw_pool")
         nc.sync.dma_start(kw_pool[:].bitcast(I32), k_words[0].rearrange("p t b -> p (t b)").bitcast(I32))
-        groups = k_scales.rearrange("o (g r) t -> (o g) r t", r=4).bitcast(I32)
-        for g in range(2):
-            nc.scalar.dma_start(ks_pool[g * QUAD:g * QUAD + 16, :].bitcast(I32), groups[g:8:2])
-        for g in range(2, 4):
-            nc.sync.dma_start(ks_pool[g * QUAD:g * QUAD + 4, :].bitcast(I32), groups[g])
+        for g in range(4):
+            nc.sync.dma_start(ks_pool[g * QUAD:g * QUAD + 8, :].bitcast(I32), k_scales[:, 4 * g:4 * g + 4, :].bitcast(I32))
 
-        quad_start = tile([P, 1], F32, "quad_start", "quad_then_queries")
+        ones = tile([P, P], F32, "ones")
+        nc.gpsimd.memset(ones[:], 1.0)
+        nc.gpsimd.memset(kb_pool[0:ROW, :], 0.0)
+        ks_second = tile([P, N], U8, "ks_second")
+        nc.gpsimd.memset(ks_second[3 * QUAD:P, :].bitcast(I32), 0)
+        quad_start = tile([P, 1], F32, "quad_start")
         column = tile([P, P], F32, "column")
         nc.vector.tensor_tensor_scan(column[:], ones[:], ones[:], -1.0, ALU.mult, ALU.add)
         for g in range(P // QUAD):
             nc.vector.memset(quad_start[g * QUAD:(g + 1) * QUAD, :], float(g * QUAD))
-        in_quad = tile([P, QUAD], F32, "in_quad", "in_quad_then_plane")
+        in_quad = tile([P, QUAD], F32, "in_quad")
         nc.vector.transpose(in_quad[:], column[:, 0:QUAD])
+        position = tile([P, 1], F32, "position")
+        nc.scalar.activation(position[:], in_quad[:, 0:1], ACT.Identity, bias=quad_start[:])
         ident = tile([P, P], F32, "ident")
-        nc.vector.tensor_scalar(out=ident[:], in0=column[:], scalar1=quad_start[:], scalar2=in_quad[:, 0:1],
-                                op0=ALU.subtract, op1=ALU.is_equal)
-        warm = tile([P, 1], F32, "warm", "warm_then_vs")
-        nc.scalar.activation(warm[:], ident[:, 0:1], ACT.Exp)
+        nc.vector.tensor_scalar(out=ident[:], in0=column[:], scalar1=position[:], scalar2=None, op0=ALU.is_equal)
 
-        v_low = tile([P, T], F32, "v_low", "ones_then_values")
+        v_low = tile([P, T], F32, "v_low")
         nc.sync.dma_start(v_low[:], vT[0:P, :])
-        q_codes = tile([P, PASSES, NQ], U32, "q_codes", "quad_then_queries")
+        q_codes = tile([P, PASSES, NQ], U32, "q_codes")
         nc.sync.dma_start(q_codes[:].bitcast(I32), q_words[0].rearrange("o p q b -> p o (q b)").bitcast(I32))
-        q_plane = tile([P, PASSES, NQ], U8, "q_plane", "in_quad_then_plane")
+        q_plane = tile([P, PASSES, NQ], U8, "q_plane")
         nc.vector.memset(q_plane[:].rearrange("p o t -> p (o t)").bitcast(I32), 0)
-        for r in range(4):
-            nc.sync.dma_start(q_plane[r:P:QUAD, :, :].bitcast(I32),
-                              q_scales[0][:, r:16:4, :].rearrange("o f t -> f o t").bitcast(I32))
-        vs_pool = tile([P, T], F32, "vs_pool", "warm_then_vs")
+        for g in range(4):
+            nc.sync.dma_start(q_plane[g * QUAD:g * QUAD + 4, :, :].bitcast(I32),
+                              q_scales[0][:, 4 * g:4 * g + 4, :].rearrange("o r t -> r o t").bitcast(I32))
+        vs_pool = tile([P, T], F32, "vs_pool")
         nc.sync.dma_start(vs_pool[:], vs)
 
         kb_listed = tile([P, N], F32, "kb_listed", "kb_then_values")
@@ -87,16 +83,16 @@ def tile_attend_soft_cap_kb_srtq256n512t1024_kernel(tc, q_words, q_scales, k_wor
 
         ks_listed = tile([P, N], U8, "ks_listed", "kb_then_scales")
         nc.vector.tensor_copy(ks_listed[:], ks_pool[:].indirect(offsets[:]))
-        for half, source in enumerate((8, 12)):
-            nc.sync.dma_start(ks_second[half * 64:(half + 1) * 64, :].bitcast(I32),
-                              ks_listed[source:source + 64, :].bitcast(I32))
+        for first, count in ((0, 64), (64, 32), (96, 16)):
+            nc.sync.dma_start(ks_second[first:first + count, :].bitcast(I32),
+                              ks_listed[first + 4:first + 4 + count, :].bitcast(I32))
         planes = (ks_listed, ks_second)
         v_high = tile([P, T], F32, "v_high", "kb_then_values")
         nc.sync.dma_start(v_high[:], vT[P:2 * P, :])
 
         v_rounded = tile([P, T], BF16, "v_rounded")
         nc.scalar.copy(v_rounded[:], v_low[:])
-        kb_half = tile([P, 4], F32, "kb_half", "ones_then_values")
+        kb_half = tile([P, 4], F32, "kb_half", "bias_then_values")
         nc.scalar.activation(kb_half[:], kb_turned[:, :, ROW], ACT.Copy, scale=1.0 / CAP)
         v_listed_low = tile([P, N], BF16, "v_listed_low")
         nc.scalar.activation(v_listed_low[:], v_rounded[:].indirect(offsets[:]), ACT.Copy)
@@ -139,7 +135,7 @@ def tile_attend_soft_cap_kb_srtq256n512t1024_kernel(tc, q_words, q_scales, k_wor
         nc.vector.tensor_copy(vs_listed[:], vs_pool[:].indirect(offsets[:]))
         v_rounded_high = tile([P, T], BF16, "v_rounded_high")
         nc.vector.tensor_copy(v_rounded_high[:], v_high[:])
-        v_listed_high = tile([P, N], BF16, "v_listed_high", "ones_then_values")
+        v_listed_high = tile([P, N], BF16, "v_listed_high", "bias_then_values")
         nc.scalar.activation(v_listed_high[:], v_rounded_high[:].indirect(offsets[:]), ACT.Copy)
 
         neg_m = []
@@ -160,8 +156,8 @@ def tile_attend_soft_cap_kb_srtq256n512t1024_kernel(tc, q_words, q_scales, k_wor
         for qb in range(2):
             p = tile([P, 2, P, 2], F32, "p%d" % qb)
             l = tile([P, 1], F32, "l%d" % qb)
-            nc.scalar.activation(p[:], turned[qb][:].rearrange("q (u m r) -> q u m r", u=2, r=2), ACT.Exp,
-                                 bias=neg_m[qb][:], scale=CAP, accum_out=l[:])
+            nc.scalar.activation(p[:].rearrange("q u m r -> q (u m r)"), neg_c[:, qb, :], ACT.Exp,
+                                 bias=neg_m[qb][:], scale=-1.0, accum_out=l[:])
             w = tile([P, 2, P, 2], BF16, "w%d" % qb)
             for u in range(2):
                 nc.vector.tensor_tensor(w[:, u], p[:, u], vs_listed[:].rearrange("q (m u r) -> q u m r", u=2, r=2)[:, u],

@@ -27,6 +27,7 @@ def tile_attend_soft_cap_kb_srtq256n512t1024_kernel(tc, q_words, q_scales, k_wor
     nc = tc.nc
     with ExitStack() as ctx:
         sb = ctx.enter_context(tc.tile_pool(name="sb", bufs=1))
+        placed = ctx.enter_context(tc.tile_pool(name="placed", bufs=1))
         ps = ctx.enter_context(tc.psum_pool(name="ps", bufs=1))
 
         def tile(shape, dtype, name, tag=None):
@@ -36,18 +37,19 @@ def tile_attend_soft_cap_kb_srtq256n512t1024_kernel(tc, q_words, q_scales, k_wor
             return ps.tile(shape, F32, name=name, tag="bank%d" % number)
 
         offsets = sb.tile([P, N // 16], U16, name="offsets")
-        ks_pool = tile([P, T], U8, "ks_pool", "ks_then_words")
-        nc.vector.memset(ks_pool[:].bitcast(I32), 0)
+        ks_pool = placed.tile([P, T], U8, name="ks_pool", offset=3 * N)
+        ones = tile([P, P], F32, "ones", "ones_then_values")
+        nc.gpsimd.memset(ones[:], 1.0)
+        nc.gpsimd.memset(ks_pool[:].bitcast(I32), 0)
         nc.sync.dma_start(offsets[:], offs)
         kb_pool = tile([P, T], F32, "kb_pool", "kb_then_scales")
-        nc.sync.dma_start(kb_pool[ROW:P, :], kb[0:1, :])
+        nc.scalar.dma_start(kb_pool[ROW:P, :], kb[0:1, :])
         kw_pool = tile([P, T], U32, "kw_pool")
         nc.sync.dma_start(kw_pool[:].bitcast(I32), k_words[0].rearrange("p t b -> p (t b)").bitcast(I32))
-        for g in range(4):
-            nc.sync.dma_start(ks_pool[g * QUAD:g * QUAD + 8, :].bitcast(I32), k_scales[:, 4 * g:4 * g + 4, :].bitcast(I32))
+        for r in range(4):
+            queue = (nc.scalar, nc.sync)[r // 2]
+            queue.dma_start(ks_pool[r:P:16, :].bitcast(I32), k_scales[:, r:16:4, :].rearrange("o g t -> g o t").bitcast(I32))
 
-        ones = tile([P, P], F32, "ones")
-        nc.gpsimd.memset(ones[:], 1.0)
         nc.gpsimd.memset(kb_pool[0:ROW, :], 0.0)
         ks_second = tile([P, N], U8, "ks_second")
         nc.gpsimd.memset(ks_second[3 * QUAD:P, :].bitcast(I32), 0)
@@ -56,26 +58,29 @@ def tile_attend_soft_cap_kb_srtq256n512t1024_kernel(tc, q_words, q_scales, k_wor
         nc.vector.tensor_tensor_scan(column[:], ones[:], ones[:], -1.0, ALU.mult, ALU.add)
         for g in range(P // QUAD):
             nc.vector.memset(quad_start[g * QUAD:(g + 1) * QUAD, :], float(g * QUAD))
-        in_quad = tile([P, QUAD], F32, "in_quad")
+        in_quad = tile([P, QUAD], F32, "in_quad", "in_quad_then_plane")
         nc.vector.transpose(in_quad[:], column[:, 0:QUAD])
-        position = tile([P, 1], F32, "position")
-        nc.scalar.activation(position[:], in_quad[:, 0:1], ACT.Identity, bias=quad_start[:])
+        apart = tile([P, P], F32, "apart")
+        nc.vector.tensor_scalar(out=apart[:], in0=column[:], scalar1=quad_start[:], scalar2=in_quad[:, 0:1],
+                                op0=ALU.subtract, op1=ALU.subtract)
+        squared = placed.tile([P, P], F32, name="squared", offset=16 * N - 2 * P)
+        nc.vector.tensor_tensor(squared[:], apart[:], apart[:], ALU.mult)
         ident = tile([P, P], F32, "ident")
-        nc.vector.tensor_scalar(out=ident[:], in0=column[:], scalar1=position[:], scalar2=None, op0=ALU.is_equal)
+        nc.scalar.activation(ident[:], squared[:], ACT.Relu, bias=1.0, scale=-1.0)
 
-        v_low = tile([P, T], F32, "v_low")
+        v_low = tile([P, T], F32, "v_low", "ones_then_values")
         nc.sync.dma_start(v_low[:], vT[0:P, :])
-        q_codes = tile([P, PASSES, NQ], U32, "q_codes")
-        nc.sync.dma_start(q_codes[:].bitcast(I32), q_words[0].rearrange("o p q b -> p o (q b)").bitcast(I32))
-        q_plane = tile([P, PASSES, NQ], U8, "q_plane")
+        q_plane = tile([P, PASSES, NQ], U8, "q_plane", "in_quad_then_plane")
         nc.vector.memset(q_plane[:].rearrange("p o t -> p (o t)").bitcast(I32), 0)
-        for g in range(4):
-            nc.sync.dma_start(q_plane[g * QUAD:g * QUAD + 4, :, :].bitcast(I32),
-                              q_scales[0][:, 4 * g:4 * g + 4, :].rearrange("o r t -> r o t").bitcast(I32))
-        vs_pool = tile([P, T], F32, "vs_pool")
+        for r in range(4):
+            nc.sync.dma_start(q_plane[r:P:QUAD, :, :].bitcast(I32),
+                              q_scales[0][:, r:16:4, :].rearrange("o f t -> f o t").bitcast(I32))
+        q_codes = placed.tile([P, PASSES, NQ], U32, name="q_codes", offset=12 * N, align_bytes=64)
+        nc.sync.dma_start(q_codes[:].bitcast(I32), q_words[0].rearrange("o p q b -> p o (q b)").bitcast(I32))
+        vs_pool = placed.tile([P, T], F32, name="vs_pool", offset=16 * N)
         nc.sync.dma_start(vs_pool[:], vs)
 
-        kb_listed = tile([P, N], F32, "kb_listed", "kb_then_values")
+        kb_listed = tile([P, N], F32, "kb_listed")
         nc.vector.tensor_copy(kb_listed[:], kb_pool[:].indirect(offsets[:]))
         kb_turned = bank(0, [P, 4, P], "kb_turned")
         for j in range(4):
@@ -85,31 +90,33 @@ def tile_attend_soft_cap_kb_srtq256n512t1024_kernel(tc, q_words, q_scales, k_wor
         nc.vector.tensor_copy(ks_listed[:], ks_pool[:].indirect(offsets[:]))
         for first, count in ((0, 64), (64, 32), (96, 16)):
             nc.sync.dma_start(ks_second[first:first + count, :].bitcast(I32),
-                              ks_listed[first + 4:first + 4 + count, :].bitcast(I32))
+                              ks_listed[first + 16:first + 16 + count, :].bitcast(I32))
         planes = (ks_listed, ks_second)
-        v_high = tile([P, T], F32, "v_high", "kb_then_values")
-        nc.sync.dma_start(v_high[:], vT[P:2 * P, :])
+        v_high = placed.tile([P, T], F32, name="v_high", offset=4 * N)
+        for c in range(2):
+            nc.sync.dma_start(v_high[:, c * T // 2:(c + 1) * T // 2], vT[P:2 * P, c * T // 2:(c + 1) * T // 2])
 
         v_rounded = tile([P, T], BF16, "v_rounded")
         nc.scalar.copy(v_rounded[:], v_low[:])
-        kb_half = tile([P, 4], F32, "kb_half", "bias_then_values")
+        kb_half = tile([P, 4], F32, "kb_half", "ones_then_values")
         nc.scalar.activation(kb_half[:], kb_turned[:, :, ROW], ACT.Copy, scale=1.0 / CAP)
         v_listed_low = tile([P, N], BF16, "v_listed_low")
         nc.scalar.activation(v_listed_low[:], v_rounded[:].indirect(offsets[:]), ACT.Copy)
 
         scores = {}
-        k_pairs = tile([P, N], U32, "k_pairs")
+        k_pairs = placed.tile([P, N], U32, name="k_pairs", offset=0)
         nc.vector.tensor_copy(k_pairs[:], kw_pool[:].indirect(offsets[:]))
-        k_codes = tile([P, PASSES, N], U16, "k_codes", "ks_then_words")
+        k_codes = []
         for h in range(2):
             slots = slice(h * N // 2, (h + 1) * N // 2)
-            nc.vector.tensor_copy(k_codes[:, :, slots],
+            k_codes.append(tile([P, PASSES, N // 2], U16, "k_codes%d" % h))
+            nc.vector.tensor_copy(k_codes[h][:],
                                   k_pairs[:, slots].bitcast(U16).rearrange("p (n o) -> p o n", o=PASSES))
 
         def score_pass(j, qb, o):
             rows = slice(qb * P, (qb + 1) * P)
             nc.tensor.matmul_mx(
-                out=scores[j, qb][:], lhsT=k_codes[:, o, j * P:(j + 1) * P].bitcast(FP4X4),
+                out=scores[j, qb][:], lhsT=k_codes[j // 2][:, o, (j % 2) * P:(j % 2 + 1) * P].bitcast(FP4X4),
                 lhsT_scale=planes[o][:, j * P:(j + 1) * P],
                 rhs=q_codes[:, o, rows].bitcast(FP8X4), rhs_scale=q_plane[:, o, rows],
                 start=(o == 0), stop=(o == PASSES - 1))
@@ -131,15 +138,16 @@ def tile_attend_soft_cap_kb_srtq256n512t1024_kernel(tc, q_words, q_scales, k_wor
                 dealt = turned[qb][:].rearrange("q (u m r) -> q m u r", u=2, r=2)
                 nc.tensor.transpose(dealt[:, j * QUAD:(j + 1) * QUAD], capped[j, qb][:], ident[:])
 
-        vs_listed = tile([P, N], F32, "vs_listed")
+        vs_listed = placed.tile([P, N], F32, name="vs_listed", offset=0)
         nc.vector.tensor_copy(vs_listed[:], vs_pool[:].indirect(offsets[:]))
         v_rounded_high = tile([P, T], BF16, "v_rounded_high")
-        nc.vector.tensor_copy(v_rounded_high[:], v_high[:])
-        v_listed_high = tile([P, N], BF16, "v_listed_high", "bias_then_values")
+        for c in range(2):
+            nc.vector.tensor_copy(v_rounded_high[:, c * T // 2:(c + 1) * T // 2], v_high[:, c * T // 2:(c + 1) * T // 2])
+        v_listed_high = tile([P, N], BF16, "v_listed_high", "ones_then_values")
         nc.scalar.activation(v_listed_high[:], v_rounded_high[:].indirect(offsets[:]), ACT.Copy)
 
         neg_m = []
-        neg_c = tile([P, 2, N], F32, "neg_c", "kb_then_values")
+        neg_c = placed.tile([P, 2, N], F32, name="neg_c", offset=4 * N)
         for qb in range(2):
             m = tile([P, 1], F32, "neg_m%d" % qb)
             nc.vector.tensor_scalar(out=neg_c[:, qb, :], in0=turned[qb][:], scalar1=-CAP, scalar2=None,

@@ -66,7 +66,7 @@ def tile_attend_soft_cap_kb_srtq256n512t1024_kernel(tc, q_words, q_scales, k_wor
         squared = placed.tile([P, P], F32, name="squared", offset=16 * N - 2 * P)
         nc.vector.tensor_tensor(squared[:], apart[:], apart[:], ALU.mult)
         ident = tile([P, P], F32, "ident")
-        nc.scalar.activation(ident[:], squared[:], ACT.Relu, bias=1.0, scale=-1.0)
+        nc.scalar.activation(ident[:], squared[:], ACT.Exp, scale=-4096.0)
 
         v_low = tile([P, T], F32, "v_low", "ones_then_values")
         nc.sync.dma_start(v_low[:], vT[0:P, :])
@@ -88,7 +88,7 @@ def tile_attend_soft_cap_kb_srtq256n512t1024_kernel(tc, q_words, q_scales, k_wor
 
         ks_listed = tile([P, N], U8, "ks_listed", "kb_then_scales")
         nc.vector.tensor_copy(ks_listed[:], ks_pool[:].indirect(offsets[:]))
-        for first, count in ((0, 64), (64, 32), (96, 16)):
+        for first, count in ((0, 64), (64, 48)):
             nc.sync.dma_start(ks_second[first:first + count, :].bitcast(I32),
                               ks_listed[first + 16:first + 16 + count, :].bitcast(I32))
         planes = (ks_listed, ks_second)

@@ -88,13 +88,12 @@ def tile_attend_soft_cap_kb_srtq256n512t1024_kernel(tc, q_words, q_scales, k_wor
 
         ks_listed = tile([P, N], U8, "ks_listed", "kb_then_scales")
         nc.vector.tensor_copy(ks_listed[:], ks_pool[:].indirect(offsets[:]))
-        for first, count in ((0, 64), (64, 48)):
+        for first, count in ((0, 64), (64, 32), (96, 16)):
             nc.sync.dma_start(ks_second[first:first + count, :].bitcast(I32),
                               ks_listed[first + 16:first + 16 + count, :].bitcast(I32))
         planes = (ks_listed, ks_second)
         v_high = placed.tile([P, T], F32, name="v_high", offset=4 * N)
-        for c in range(2):
-            nc.sync.dma_start(v_high[:, c * T // 2:(c + 1) * T // 2], vT[P:2 * P, c * T // 2:(c + 1) * T // 2])
+        nc.sync.dma_start(v_high[:], vT[P:2 * P, :])
 
         v_rounded = tile([P, T], BF16, "v_rounded")
         nc.scalar.copy(v_rounded[:], v_low[:])
@@ -140,14 +139,11 @@ def tile_attend_soft_cap_kb_srtq256n512t1024_kernel(tc, q_words, q_scales, k_wor
 
         vs_listed = placed.tile([P, N], F32, name="vs_listed", offset=0)
         nc.vector.tensor_copy(vs_listed[:], vs_pool[:].indirect(offsets[:]))
-        v_rounded_high = tile([P, T], BF16, "v_rounded_high")
-        for c in range(2):
-            nc.vector.tensor_copy(v_rounded_high[:, c * T // 2:(c + 1) * T // 2], v_high[:, c * T // 2:(c + 1) * T // 2])
         v_listed_high = tile([P, N], BF16, "v_listed_high", "ones_then_values")
-        nc.scalar.activation(v_listed_high[:], v_rounded_high[:].indirect(offsets[:]), ACT.Copy)
+        nc.scalar.activation(v_listed_high[:], v_high[:].indirect(offsets[:]), ACT.Copy)
 
         neg_m = []
-        neg_c = placed.tile([P, 2, N], F32, name="neg_c", offset=4 * N)
+        neg_c = tile([P, 2, N], F32, "neg_c")
         for qb in range(2):
             m = tile([P, 1], F32, "neg_m%d" % qb)
             nc.vector.tensor_scalar(out=neg_c[:, qb, :], in0=turned[qb][:], scalar1=-CAP, scalar2=None,

@@ -38,14 +38,10 @@ def tile_attend_soft_cap_kb_srtq256n512t1024_kernel(tc, q_words, q_scales, k_wor
 
         offsets = sb.tile([P, N // 16], U16, name="offsets")
         ks_pool = placed.tile([P, T], U8, name="ks_pool", offset=3 * N)
-        ones = tile([P, P], F32, "ones", "ones_then_values")
-        nc.gpsimd.memset(ones[:], 1.0)
         nc.gpsimd.memset(ks_pool[:].bitcast(I32), 0)
         nc.sync.dma_start(offsets[:], offs)
-        kb_pool = tile([P, T], F32, "kb_pool", "kb_then_scales")
+        kb_pool = tile([P, T], F32, "kb_pool")
         nc.scalar.dma_start(kb_pool[ROW:P, :], kb[0:1, :])
-        kw_pool = tile([P, T], U32, "kw_pool")
-        nc.sync.dma_start(kw_pool[:].bitcast(I32), k_words[0].rearrange("p t b -> p (t b)").bitcast(I32))
         for r in range(4):
             queue = (nc.scalar, nc.sync)[r // 2]
             queue.dma_start(ks_pool[r:P:16, :].bitcast(I32), k_scales[:, r:16:4, :].rearrange("o g t -> g o t").bitcast(I32))
@@ -53,25 +49,29 @@ def tile_attend_soft_cap_kb_srtq256n512t1024_kernel(tc, q_words, q_scales, k_wor
         nc.gpsimd.memset(kb_pool[0:ROW, :], 0.0)
         ks_second = tile([P, N], U8, "ks_second")
         nc.gpsimd.memset(ks_second[3 * QUAD:P, :].bitcast(I32), 0)
-        quad_start = tile([P, 1], F32, "quad_start")
+        one = tile([P, 1], F32, "one", "one_then_words")
+        nc.vector.memset(one[:], 1.0)
         column = tile([P, P], F32, "column")
-        nc.vector.tensor_tensor_scan(column[:], ones[:], ones[:], -1.0, ALU.mult, ALU.add)
+        ones = one[:].to_broadcast([P, P])
+        nc.vector.tensor_tensor_scan(column[:], ones, ones, -1.0, ALU.mult, ALU.add)
+        kw_pool = tile([P, T], U32, "kw_pool", "one_then_words")
+        nc.sync.dma_start(kw_pool[:].bitcast(I32), k_words[0].rearrange("p t b -> p (t b)").bitcast(I32))
+        quad_start = tile([P, 1], F32, "quad_start", "quad_start_then_values")
         for g in range(P // QUAD):
-            nc.vector.memset(quad_start[g * QUAD:(g + 1) * QUAD, :], float(g * QUAD))
-        in_quad = tile([P, QUAD], F32, "in_quad", "in_quad_then_plane")
+            nc.vector.memset(quad_start[g * QUAD:(g + 1) * QUAD, :], float(-g * QUAD))
+        in_quad = placed.tile([P, QUAD], F32, name="in_quad", offset=16 * N - 2 * QUAD, align_bytes=64)
         nc.vector.transpose(in_quad[:], column[:, 0:QUAD])
-        apart = tile([P, P], F32, "apart")
-        nc.vector.tensor_scalar(out=apart[:], in0=column[:], scalar1=quad_start[:], scalar2=in_quad[:, 0:1],
-                                op0=ALU.subtract, op1=ALU.subtract)
-        squared = placed.tile([P, P], F32, name="squared", offset=16 * N - 2 * P)
-        nc.vector.tensor_tensor(squared[:], apart[:], apart[:], ALU.mult)
+        neg_partition = tile([P, 1], F32, "neg_partition")
+        nc.vector.tensor_tensor(neg_partition[:], quad_start[:], in_quad[:, 0:1], ALU.subtract)
+        squared = tile([P, P], F32, "squared")
+        nc.scalar.activation(squared[:], column[:], ACT.Square, bias=neg_partition[:])
         ident = tile([P, P], F32, "ident")
         nc.scalar.activation(ident[:], squared[:], ACT.Exp, scale=-4096.0)
 
-        v_low = tile([P, T], F32, "v_low", "ones_then_values")
+        v_low = tile([P, T], F32, "v_low", "quad_start_then_values")
         nc.sync.dma_start(v_low[:], vT[0:P, :])
-        q_plane = tile([P, PASSES, NQ], U8, "q_plane", "in_quad_then_plane")
-        nc.vector.memset(q_plane[:].rearrange("p o t -> p (o t)").bitcast(I32), 0)
+        q_plane = tile([P, PASSES, NQ], U8, "q_plane")
+        nc.gpsimd.memset(q_plane[:].rearrange("p o t -> p (o t)").bitcast(I32), 0)
         for r in range(4):
             nc.sync.dma_start(q_plane[r:P:QUAD, :, :].bitcast(I32),
                               q_scales[0][:, r:16:4, :].rearrange("o f t -> f o t").bitcast(I32))
@@ -81,12 +81,12 @@ def tile_attend_soft_cap_kb_srtq256n512t1024_kernel(tc, q_words, q_scales, k_wor
         nc.sync.dma_start(vs_pool[:], vs)
 
         kb_listed = tile([P, N], F32, "kb_listed")
-        nc.vector.tensor_copy(kb_listed[:], kb_pool[:].indirect(offsets[:]))
+        nc.scalar.activation(kb_listed[:], kb_pool[:].indirect(offsets[:]), ACT.Copy)
         kb_turned = bank(0, [P, 4, P], "kb_turned")
         for j in range(4):
             nc.tensor.transpose(kb_turned[:, j, :], kb_listed[:, j * P:(j + 1) * P], ident[:])
 
-        ks_listed = tile([P, N], U8, "ks_listed", "kb_then_scales")
+        ks_listed = tile([P, N], U8, "ks_listed")
         nc.vector.tensor_copy(ks_listed[:], ks_pool[:].indirect(offsets[:]))
         for first, count in ((0, 64), (64, 32), (96, 16)):
             nc.sync.dma_start(ks_second[first:first + count, :].bitcast(I32),
@@ -95,12 +95,10 @@ def tile_attend_soft_cap_kb_srtq256n512t1024_kernel(tc, q_words, q_scales, k_wor
         v_high = placed.tile([P, T], F32, name="v_high", offset=4 * N)
         nc.sync.dma_start(v_high[:], vT[P:2 * P, :])
 
-        v_rounded = tile([P, T], BF16, "v_rounded")
-        nc.scalar.copy(v_rounded[:], v_low[:])
-        kb_half = tile([P, 4], F32, "kb_half", "ones_then_values")
+        kb_half = tile([P, 4], F32, "kb_half")
         nc.scalar.activation(kb_half[:], kb_turned[:, :, ROW], ACT.Copy, scale=1.0 / CAP)
         v_listed_low = tile([P, N], BF16, "v_listed_low")
-        nc.scalar.activation(v_listed_low[:], v_rounded[:].indirect(offsets[:]), ACT.Copy)
+        nc.scalar.activation(v_listed_low[:], v_low[:].indirect(offsets[:]), ACT.Copy)
 
         scores = {}
         k_pairs = placed.tile([P, N], U32, name="k_pairs", offset=0)
@@ -125,25 +123,26 @@ def tile_attend_soft_cap_kb_srtq256n512t1024_kernel(tc, q_words, q_scales, k_wor
                 scores[j, qb] = bank(7 - 2 * j - qb, [P, P], "scores%d_%d" % (j, qb))
                 score_pass(j, qb, 0)
         capped = {}
+        all_capped = tile([P, 2 * 4, P], F32, "all_capped", "quad_start_then_values")
         for qb in range(2):
             for j in range(4):
                 score_pass(j, qb, 1)
-                capped[j, qb] = tile([P, P], F32, "tanh%d_%d" % (j, qb))
-                nc.scalar.activation(capped[j, qb][:], scores[j, qb][:], ACT.Tanh,
+                capped[j, qb] = all_capped[:, 4 * qb + j, :]
+                nc.scalar.activation(capped[j, qb], scores[j, qb][:], ACT.Tanh,
                                      bias=kb_half[:, j:j + 1], scale=1.0 / CAP)
         turned = [bank((7, 1)[qb], [P, N], "turned%d" % qb) for qb in range(2)]
         for qb in range(2):
             for j in range(4):
                 dealt = turned[qb][:].rearrange("q (u m r) -> q m u r", u=2, r=2)
-                nc.tensor.transpose(dealt[:, j * QUAD:(j + 1) * QUAD], capped[j, qb][:], ident[:])
+                nc.tensor.transpose(dealt[:, j * QUAD:(j + 1) * QUAD], capped[j, qb], ident[:])
 
         vs_listed = placed.tile([P, N], F32, name="vs_listed", offset=0)
         nc.vector.tensor_copy(vs_listed[:], vs_pool[:].indirect(offsets[:]))
-        v_listed_high = tile([P, N], BF16, "v_listed_high", "ones_then_values")
-        nc.scalar.activation(v_listed_high[:], v_high[:].indirect(offsets[:]), ACT.Copy)
+        v_listed_high = tile([P, N], BF16, "v_listed_high")
+        nc.vector.tensor_copy(v_listed_high[:], v_high[:].indirect(offsets[:]))
 
         neg_m = []
-        neg_c = tile([P, 2, N], F32, "neg_c")
+        neg_c = placed.tile([P, 2, N], F32, name="neg_c", offset=4 * N)
         for qb in range(2):
             m = tile([P, 1], F32, "neg_m%d" % qb)
             nc.vector.tensor_scalar(out=neg_c[:, qb, :], in0=turned[qb][:], scalar1=-CAP, scalar2=None,

@@ -42,43 +42,46 @@ def tile_attend_soft_cap_kb_srtq256n512t1024_kernel(tc, q_words, q_scales, k_wor
         nc.sync.dma_start(offsets[:], offs)
         kb_pool = tile([P, T], F32, "kb_pool")
         nc.scalar.dma_start(kb_pool[ROW:P, :], kb[0:1, :])
+        vs_pool = tile([P, T], F32, "vs_pool")
+        nc.scalar.dma_start(vs_pool[ROW:P, :], vs[0:1, :])
         for r in range(4):
-            queue = (nc.scalar, nc.sync)[r // 2]
+            queue = nc.sync if r else nc.scalar
             queue.dma_start(ks_pool[r:P:16, :].bitcast(I32), k_scales[:, r:16:4, :].rearrange("o g t -> g o t").bitcast(I32))
 
         nc.gpsimd.memset(kb_pool[0:ROW, :], 0.0)
-        ks_second = tile([P, N], U8, "ks_second")
-        nc.gpsimd.memset(ks_second[3 * QUAD:P, :].bitcast(I32), 0)
         one = tile([P, 1], F32, "one", "one_then_words")
         nc.vector.memset(one[:], 1.0)
-        column = tile([P, P], F32, "column")
+        column = tile([P, P], F32, "column", "column_then_values")
         ones = one[:].to_broadcast([P, P])
         nc.vector.tensor_tensor_scan(column[:], ones, ones, -1.0, ALU.mult, ALU.add)
         kw_pool = tile([P, T], U32, "kw_pool", "one_then_words")
         nc.sync.dma_start(kw_pool[:].bitcast(I32), k_words[0].rearrange("p t b -> p (t b)").bitcast(I32))
-        quad_start = tile([P, 1], F32, "quad_start", "quad_start_then_values")
+        quad_start = tile([P, 1], F32, "quad_start")
         for g in range(P // QUAD):
             nc.vector.memset(quad_start[g * QUAD:(g + 1) * QUAD, :], float(-g * QUAD))
         in_quad = placed.tile([P, QUAD], F32, name="in_quad", offset=16 * N - 2 * QUAD, align_bytes=64)
         nc.vector.transpose(in_quad[:], column[:, 0:QUAD])
         neg_partition = tile([P, 1], F32, "neg_partition")
         nc.vector.tensor_tensor(neg_partition[:], quad_start[:], in_quad[:, 0:1], ALU.subtract)
-        squared = tile([P, P], F32, "squared")
+        squared = tile([P, P], F32, "squared", "squared_then_values")
         nc.scalar.activation(squared[:], column[:], ACT.Square, bias=neg_partition[:])
         ident = tile([P, P], F32, "ident")
         nc.scalar.activation(ident[:], squared[:], ACT.Exp, scale=-4096.0)
 
-        v_low = tile([P, T], F32, "v_low", "quad_start_then_values")
-        nc.sync.dma_start(v_low[:], vT[0:P, :])
-        q_plane = tile([P, PASSES, NQ], U8, "q_plane")
+        q_codes = placed.tile([P, PASSES, NQ], U32, name="q_codes", offset=12 * N, align_bytes=64)
+        nc.sync.dma_start(q_codes[:].bitcast(I32), q_words[0].rearrange("o p q b -> p o (q b)").bitcast(I32))
+        q_plane = placed.tile([P, PASSES, NQ], U8, name="q_plane", offset=16 * N, align_bytes=64)
         nc.gpsimd.memset(q_plane[:].rearrange("p o t -> p (o t)").bitcast(I32), 0)
         for r in range(4):
             nc.sync.dma_start(q_plane[r:P:QUAD, :, :].bitcast(I32),
                               q_scales[0][:, r:16:4, :].rearrange("o f t -> f o t").bitcast(I32))
-        q_codes = placed.tile([P, PASSES, NQ], U32, name="q_codes", offset=12 * N, align_bytes=64)
-        nc.sync.dma_start(q_codes[:].bitcast(I32), q_words[0].rearrange("o p q b -> p o (q b)").bitcast(I32))
-        vs_pool = placed.tile([P, T], F32, name="vs_pool", offset=16 * N)
-        nc.sync.dma_start(vs_pool[:], vs)
+        v_low = tile([P, T], F32, "v_low", "column_then_values")
+        nc.sync.dma_start(v_low[:], vT[0:P, :])
+        v_high = tile([P, T], F32, "v_high", "squared_then_values")
+        nc.sync.dma_start(v_high[:], vT[P:2 * P, :])
+        nc.gpsimd.memset(vs_pool[0:ROW, :], 0.0)
+        ks_second = tile([P, N], U8, "ks_second")
+        nc.gpsimd.memset(ks_second[3 * QUAD:P, :].bitcast(I32), 0)
 
         kb_listed = tile([P, N], F32, "kb_listed")
         nc.scalar.activation(kb_listed[:], kb_pool[:].indirect(offsets[:]), ACT.Copy)
@@ -86,14 +89,18 @@ def tile_attend_soft_cap_kb_srtq256n512t1024_kernel(tc, q_words, q_scales, k_wor
         for j in range(4):
             nc.tensor.transpose(kb_turned[:, j, :], kb_listed[:, j * P:(j + 1) * P], ident[:])
 
+        vs_listed = tile([P, N], F32, "vs_listed")
+        nc.scalar.activation(vs_listed[:], vs_pool[:].indirect(offsets[:]), ACT.Copy)
+        vs_turned = bank(1, [P, 4, P], "vs_turned")
+        for j in range(4):
+            nc.tensor.transpose(vs_turned[:, j, :], vs_listed[:, j * P:(j + 1) * P], ident[:])
+
         ks_listed = tile([P, N], U8, "ks_listed")
         nc.vector.tensor_copy(ks_listed[:], ks_pool[:].indirect(offsets[:]))
         for first, count in ((0, 64), (64, 32), (96, 16)):
             nc.sync.dma_start(ks_second[first:first + count, :].bitcast(I32),
                               ks_listed[first + 16:first + 16 + count, :].bitcast(I32))
         planes = (ks_listed, ks_second)
-        v_high = placed.tile([P, T], F32, name="v_high", offset=4 * N)
-        nc.sync.dma_start(v_high[:], vT[P:2 * P, :])
 
         kb_half = tile([P, 4], F32, "kb_half")
         nc.scalar.activation(kb_half[:], kb_turned[:, :, ROW], ACT.Copy, scale=1.0 / CAP)
@@ -110,6 +117,9 @@ def tile_attend_soft_cap_kb_srtq256n512t1024_kernel(tc, q_words, q_scales, k_wor
             nc.vector.tensor_copy(k_codes[h][:],
                                   k_pairs[:, slots].bitcast(U16).rearrange("p (n o) -> p o n", o=PASSES))
 
+        vs_columns = tile([P, 4], F32, "vs_columns")
+        nc.vector.tensor_copy(vs_columns[:], vs_turned[:, :, ROW])
+
         def score_pass(j, qb, o):
             rows = slice(qb * P, (qb + 1) * P)
             nc.tensor.matmul_mx(
@@ -123,7 +133,7 @@ def tile_attend_soft_cap_kb_srtq256n512t1024_kernel(tc, q_words, q_scales, k_wor
                 scores[j, qb] = bank(7 - 2 * j - qb, [P, P], "scores%d_%d" % (j, qb))
                 score_pass(j, qb, 0)
         capped = {}
-        all_capped = tile([P, 2 * 4, P], F32, "all_capped", "quad_start_then_values")
+        all_capped = tile([P, 2 * 4, P], F32, "all_capped", "column_then_values")
         for qb in range(2):
             for j in range(4):
                 score_pass(j, qb, 1)
@@ -136,13 +146,15 @@ def tile_attend_soft_cap_kb_srtq256n512t1024_kernel(tc, q_words, q_scales, k_wor
                 dealt = turned[qb][:].rearrange("q (u m r) -> q m u r", u=2, r=2)
                 nc.tensor.transpose(dealt[:, j * QUAD:(j + 1) * QUAD], capped[j, qb], ident[:])
 
-        vs_listed = placed.tile([P, N], F32, name="vs_listed", offset=0)
-        nc.vector.tensor_copy(vs_listed[:], vs_pool[:].indirect(offsets[:]))
-        v_listed_high = tile([P, N], BF16, "v_listed_high")
+        vs_spread = bank(6, [P, N], "vs_spread")
+        for j in range(4):
+            dealt = vs_spread[:].rearrange("q (u m r) -> q m u r", u=2, r=2)
+            nc.tensor.transpose(dealt[:, j * QUAD:(j + 1) * QUAD], vs_columns[:, j:j + 1].to_broadcast([P, P]), ident[:])
+        v_listed_high = placed.tile([P, N], BF16, name="v_listed_high", offset=0)
         nc.vector.tensor_copy(v_listed_high[:], v_high[:].indirect(offsets[:]))
 
         neg_m = []
-        neg_c = placed.tile([P, 2, N], F32, name="neg_c", offset=4 * N)
+        neg_c = tile([P, 2, N], F32, "neg_c", "squared_then_values")
         for qb in range(2):
             m = tile([P, 1], F32, "neg_m%d" % qb)
             nc.vector.tensor_scalar(out=neg_c[:, qb, :], in0=turned[qb][:], scalar1=-CAP, scalar2=None,
@@ -163,7 +175,7 @@ def tile_attend_soft_cap_kb_srtq256n512t1024_kernel(tc, q_words, q_scales, k_wor
                                  bias=neg_m[qb][:], scale=-1.0, accum_out=l[:])
             w = tile([P, 2, P, 2], BF16, "w%d" % qb)
             for u in range(2):
-                nc.vector.tensor_tensor(w[:, u], p[:, u], vs_listed[:].rearrange("q (m u r) -> q u m r", u=2, r=2)[:, u],
+                nc.vector.tensor_tensor(w[:, u], p[:, u], vs_spread[:].rearrange("q (u m r) -> q u m r", u=2, r=2)[:, u],
                                         ALU.mult)
             weights.append(w)
             total.append(l)
@@ -190,7 +202,7 @@ def tile_attend_soft_cap_kb_srtq256n512t1024_kernel(tc, q_words, q_scales, k_wor
             width = DV // (qb + 1)
             for h in range(qb + 1):
                 cols = slice(h * width, (h + 1) * width)
-                sums = bank(4 + qb + h, [P, width], "sums%d_%d" % (qb, h))
+                sums = bank((4, 5, 7)[qb + h], [P, width], "sums%d_%d" % (qb, h))
                 nc.tensor.matmul_mx(out=sums[:], lhsT=w_codes[:].bitcast(FP8X4), lhsT_scale=w_plane[:],
                                     rhs=v_codes[:, cols].bitcast(FP8X4), rhs_scale=v_plane[:, cols],
                                     start=True, stop=True)

@@ -63,7 +63,7 @@ def tile_attend_soft_cap_kb_srtq256n512t1024_kernel(tc, q_words, q_scales, k_wor
         nc.vector.transpose(in_quad[:], column[:, 0:QUAD])
         neg_partition = tile([P, 1], F32, "neg_partition")
         nc.vector.tensor_tensor(neg_partition[:], quad_start[:], in_quad[:, 0:1], ALU.subtract)
-        squared = tile([P, P], F32, "squared", "squared_then_values")
+        squared = tile([P, P], F32, "squared")
         nc.scalar.activation(squared[:], column[:], ACT.Square, bias=neg_partition[:])
         ident = tile([P, P], F32, "ident")
         nc.scalar.activation(ident[:], squared[:], ACT.Exp, scale=-4096.0)
@@ -77,8 +77,6 @@ def tile_attend_soft_cap_kb_srtq256n512t1024_kernel(tc, q_words, q_scales, k_wor
                               q_scales[0][:, r:16:4, :].rearrange("o f t -> f o t").bitcast(I32))
         v_low = tile([P, T], F32, "v_low", "column_then_values")
         nc.sync.dma_start(v_low[:], vT[0:P, :])
-        v_high = tile([P, T], F32, "v_high", "squared_then_values")
-        nc.sync.dma_start(v_high[:], vT[P:2 * P, :])
         nc.gpsimd.memset(vs_pool[0:ROW, :], 0.0)
         ks_second = tile([P, N], U8, "ks_second")
         nc.gpsimd.memset(ks_second[3 * QUAD:P, :].bitcast(I32), 0)
@@ -101,6 +99,8 @@ def tile_attend_soft_cap_kb_srtq256n512t1024_kernel(tc, q_words, q_scales, k_wor
             nc.sync.dma_start(ks_second[first:first + count, :].bitcast(I32),
                               ks_listed[first + 16:first + 16 + count, :].bitcast(I32))
         planes = (ks_listed, ks_second)
+        v_high = placed.tile([P, T], F32, name="v_high", offset=4 * N)
+        nc.sync.dma_start(v_high[:], vT[P:2 * P, :])
 
         kb_half = tile([P, 4], F32, "kb_half")
         nc.scalar.activation(kb_half[:], kb_turned[:, :, ROW], ACT.Copy, scale=1.0 / CAP)
@@ -146,22 +146,22 @@ def tile_attend_soft_cap_kb_srtq256n512t1024_kernel(tc, q_words, q_scales, k_wor
                 dealt = turned[qb][:].rearrange("q (u m r) -> q m u r", u=2, r=2)
                 nc.tensor.transpose(dealt[:, j * QUAD:(j + 1) * QUAD], capped[j, qb], ident[:])
 
-        vs_spread = bank(6, [P, N], "vs_spread")
-        for j in range(4):
-            dealt = vs_spread[:].rearrange("q (u m r) -> q m u r", u=2, r=2)
-            nc.tensor.transpose(dealt[:, j * QUAD:(j + 1) * QUAD], vs_columns[:, j:j + 1].to_broadcast([P, P]), ident[:])
         v_listed_high = placed.tile([P, N], BF16, name="v_listed_high", offset=0)
         nc.vector.tensor_copy(v_listed_high[:], v_high[:].indirect(offsets[:]))
 
         neg_m = []
-        neg_c = tile([P, 2, N], F32, "neg_c", "squared_then_values")
+        neg_c = placed.tile([P, 2, N], F32, name="neg_c", offset=4 * N)
         for qb in range(2):
             m = tile([P, 1], F32, "neg_m%d" % qb)
             nc.vector.tensor_scalar(out=neg_c[:, qb, :], in0=turned[qb][:], scalar1=-CAP, scalar2=None,
                                     op0=ALU.mult, op1=ALU.min, accum_out=m[:])
             neg_m.append(m)
 
-        v_turned = bank(0, [P, 2, P, 2], "v_turned")
+        vs_spread = bank(7, [P, N], "vs_spread")
+        for j in range(4):
+            dealt = vs_spread[:].rearrange("q (u m r) -> q m u r", u=2, r=2)
+            nc.tensor.transpose(dealt[:, j * QUAD:(j + 1) * QUAD], vs_columns[:, j:j + 1].to_broadcast([P, P]), ident[:])
+        v_turned = bank(1, [P, 2, P, 2], "v_turned")
         for h, listed in enumerate((v_listed_low, v_listed_high)):
             words = listed[:].bitcast(F32)
             for u in range(2):
@@ -202,7 +202,7 @@ def tile_attend_soft_cap_kb_srtq256n512t1024_kernel(tc, q_words, q_scales, k_wor
             width = DV // (qb + 1)
             for h in range(qb + 1):
                 cols = slice(h * width, (h + 1) * width)
-                sums = bank((4, 5, 7)[qb + h], [P, width], "sums%d_%d" % (qb, h))
+                sums = bank(4 + qb + h, [P, width], "sums%d_%d" % (qb, h))
                 nc.tensor.matmul_mx(out=sums[:], lhsT=w_codes[:].bitcast(FP8X4), lhsT_scale=w_plane[:],
                                     rhs=v_codes[:, cols].bitcast(FP8X4), rhs_scale=v_plane[:, cols],
                                     start=True, stop=True)

from contextlib import ExitStack

import concourse.mybir as mybir

N, T, D, DV, NQ = 512, 1024, 1024, 256, 256
CAP = 2.0
FLOPS = 2 * NQ * N * D + 2 * NQ * N * DV

F32 = mybir.dt.float32
BF16 = mybir.dt.bfloat16
I32 = mybir.dt.int32
U32 = mybir.dt.uint32
U16 = mybir.dt.uint16
U8 = mybir.dt.uint8
FP8X4 = mybir.dt.float8_e4m3fn_x4
FP4X4 = mybir.dt.float4_e2m1fn_x4
ACT = mybir.ActivationFunctionType
ALU = mybir.AluOpType

P = 128
QUAD = 32
PASSES = D // 512
ROW = P - 1


def tile_attend_soft_cap_kb_srtq256n512t1024_kernel(tc, q_words, q_scales, k_words, k_scales, vT, vs, kb, offs, out):
    nc = tc.nc
    with ExitStack() as ctx:
        sb = ctx.enter_context(tc.tile_pool(name="sb", bufs=1))
        placed = ctx.enter_context(tc.tile_pool(name="placed", bufs=1))
        ps = ctx.enter_context(tc.psum_pool(name="ps", bufs=1))

        def tile(shape, dtype, name, tag=None):
            return sb.tile(shape, dtype, name=name, tag=tag or name, align_bytes=64)

        def bank(number, shape, name):
            return ps.tile(shape, F32, name=name, tag="bank%d" % number)

        offsets = sb.tile([P, N // 16], U16, name="offsets")
        ks_pool = placed.tile([P, T], U8, name="ks_pool", offset=3 * N)
        nc.gpsimd.memset(ks_pool[:].bitcast(I32), 0)
        nc.sync.dma_start(offsets[:], offs)
        kb_pool = tile([P, T], F32, "kb_pool")
        nc.scalar.dma_start(kb_pool[ROW:P, :], kb[0:1, :])
        vs_pool = tile([P, T], F32, "vs_pool")
        nc.scalar.dma_start(vs_pool[ROW:P, :], vs[0:1, :])
        for r in range(4):
            queue = nc.sync if r else nc.scalar
            queue.dma_start(ks_pool[r:P:16, :].bitcast(I32), k_scales[:, r:16:4, :].rearrange("o g t -> g o t").bitcast(I32))

        nc.gpsimd.memset(kb_pool[0:ROW, :], 0.0)
        one = tile([P, 1], F32, "one", "one_then_words")
        nc.vector.memset(one[:], 1.0)
        column = tile([P, P], F32, "column", "column_then_values")
        ones = one[:].to_broadcast([P, P])
        nc.vector.tensor_tensor_scan(column[:], ones, ones, -1.0, ALU.mult, ALU.add)
        kw_pool = tile([P, T], U32, "kw_pool", "one_then_words")
        nc.sync.dma_start(kw_pool[:].bitcast(I32), k_words[0].rearrange("p t b -> p (t b)").bitcast(I32))
        quad_start = tile([P, 1], F32, "quad_start")
        for g in range(P // QUAD):
            nc.vector.memset(quad_start[g * QUAD:(g + 1) * QUAD, :], float(-g * QUAD))
        in_quad = placed.tile([P, QUAD], F32, name="in_quad", offset=16 * N - 2 * QUAD, align_bytes=64)
        nc.vector.transpose(in_quad[:], column[:, 0:QUAD])
        neg_partition = tile([P, 1], F32, "neg_partition")
        nc.vector.tensor_tensor(neg_partition[:], quad_start[:], in_quad[:, 0:1], ALU.subtract)
        squared = tile([P, P], F32, "squared")
        nc.scalar.activation(squared[:], column[:], ACT.Square, bias=neg_partition[:])
        ident = tile([P, P], F32, "ident")
        nc.scalar.activation(ident[:], squared[:], ACT.Exp, scale=-4096.0)

        q_codes = placed.tile([P, PASSES, NQ], U32, name="q_codes", offset=12 * N, align_bytes=64)
        nc.sync.dma_start(q_codes[:].bitcast(I32), q_words[0].rearrange("o p q b -> p o (q b)").bitcast(I32))
        q_plane = placed.tile([P, PASSES, NQ], U8, name="q_plane", offset=16 * N, align_bytes=64)
        nc.gpsimd.memset(q_plane[:].rearrange("p o t -> p (o t)").bitcast(I32), 0)
        for r in range(4):
            nc.sync.dma_start(q_plane[r:P:QUAD, :, :].bitcast(I32),
                              q_scales[0][:, r:16:4, :].rearrange("o f t -> f o t").bitcast(I32))
        v_low = tile([P, T], F32, "v_low", "column_then_values")
        nc.sync.dma_start(v_low[:], vT[0:P, :])
        nc.gpsimd.memset(vs_pool[0:ROW, :], 0.0)
        ks_second = tile([P, N], U8, "ks_second")
        nc.gpsimd.memset(ks_second[3 * QUAD:P, :].bitcast(I32), 0)

        kb_listed = tile([P, N], F32, "kb_listed")
        nc.scalar.activation(kb_listed[:], kb_pool[:].indirect(offsets[:]), ACT.Copy)
        kb_turned = bank(0, [P, 4, P], "kb_turned")
        for j in range(4):
            nc.tensor.transpose(kb_turned[:, j, :], kb_listed[:, j * P:(j + 1) * P], ident[:])

        vs_listed = tile([P, N], F32, "vs_listed")
        nc.scalar.activation(vs_listed[:], vs_pool[:].indirect(offsets[:]), ACT.Copy)
        vs_turned = bank(1, [P, 4, P], "vs_turned")
        for j in range(4):
            nc.tensor.transpose(vs_turned[:, j, :], vs_listed[:, j * P:(j + 1) * P], ident[:])

        ks_listed = tile([P, N], U8, "ks_listed")
        nc.vector.tensor_copy(ks_listed[:], ks_pool[:].indirect(offsets[:]))
        for first, count in ((0, 64), (64, 32), (96, 16)):
            nc.sync.dma_start(ks_second[first:first + count, :].bitcast(I32),
                              ks_listed[first + 16:first + 16 + count, :].bitcast(I32))
        planes = (ks_listed, ks_second)
        v_high = placed.tile([P, T], F32, name="v_high", offset=4 * N)
        nc.sync.dma_start(v_high[:], vT[P:2 * P, :])

        kb_half = tile([P, 4], F32, "kb_half")
        nc.scalar.activation(kb_half[:], kb_turned[:, :, ROW], ACT.Copy, scale=1.0 / CAP)
        v_listed_low = tile([P, N], BF16, "v_listed_low")
        nc.scalar.activation(v_listed_low[:], v_low[:].indirect(offsets[:]), ACT.Copy)

        scores = {}
        k_pairs = placed.tile([P, N], U32, name="k_pairs", offset=0)
        nc.vector.tensor_copy(k_pairs[:], kw_pool[:].indirect(offsets[:]))
        k_codes = []
        for h in range(2):
            slots = slice(h * N // 2, (h + 1) * N // 2)
            k_codes.append(tile([P, PASSES, N // 2], U16, "k_codes%d" % h))
            nc.vector.tensor_copy(k_codes[h][:],
                                  k_pairs[:, slots].bitcast(U16).rearrange("p (n o) -> p o n", o=PASSES))

        vs_columns = tile([P, 4], F32, "vs_columns")
        nc.vector.tensor_copy(vs_columns[:], vs_turned[:, :, ROW])

        def score_pass(j, qb, o):
            rows = slice(qb * P, (qb + 1) * P)
            nc.tensor.matmul_mx(
                out=scores[j, qb][:], lhsT=k_codes[j // 2][:, o, (j % 2) * P:(j % 2 + 1) * P].bitcast(FP4X4),
                lhsT_scale=planes[o][:, j * P:(j + 1) * P],
                rhs=q_codes[:, o, rows].bitcast(FP8X4), rhs_scale=q_plane[:, o, rows],
                start=(o == 0), stop=(o == PASSES - 1))

        for j in range(4):
            for qb in range(2):
                scores[j, qb] = bank(7 - 2 * j - qb, [P, P], "scores%d_%d" % (j, qb))
                score_pass(j, qb, 0)
        capped = {}
        all_capped = tile([P, 2 * 4, P], F32, "all_capped", "column_then_values")
        for qb in range(2):
            for j in range(4):
                score_pass(j, qb, 1)
                capped[j, qb] = all_capped[:, 4 * qb + j, :]
                nc.scalar.activation(capped[j, qb], scores[j, qb][:], ACT.Tanh,
                                     bias=kb_half[:, j:j + 1], scale=1.0 / CAP)
        turned = [bank((7, 1)[qb], [P, N], "turned%d" % qb) for qb in range(2)]
        for qb in range(2):
            for j in range(4):
                dealt = turned[qb][:].rearrange("q (u m r) -> q m u r", u=2, r=2)
                nc.tensor.transpose(dealt[:, j * QUAD:(j + 1) * QUAD], capped[j, qb], ident[:])

        v_listed_high = placed.tile([P, N], BF16, name="v_listed_high", offset=0)
        nc.vector.tensor_copy(v_listed_high[:], v_high[:].indirect(offsets[:]))

        neg_m = []
        neg_c = placed.tile([P, 2, N], F32, name="neg_c", offset=4 * N)
        for qb in range(2):
            m = tile([P, 1], F32, "neg_m%d" % qb)
            nc.vector.tensor_scalar(out=neg_c[:, qb, :], in0=turned[qb][:], scalar1=-CAP, scalar2=None,
                                    op0=ALU.mult, op1=ALU.min, accum_out=m[:])
            neg_m.append(m)

        vs_spread = bank(7, [P, N], "vs_spread")
        for j in range(4):
            dealt = vs_spread[:].rearrange("q (u m r) -> q m u r", u=2, r=2)
            nc.tensor.transpose(dealt[:, j * QUAD:(j + 1) * QUAD], vs_columns[:, j:j + 1].to_broadcast([P, P]), ident[:])
        v_turned = bank(1, [P, 2, P, 2], "v_turned")
        for h, listed in enumerate((v_listed_low, v_listed_high)):
            words = listed[:].bitcast(F32)
            for u in range(2):
                nc.tensor.transpose(v_turned[:, h, :, u], words[:, u:2 * P:2], ident[:])

        weights, total = [], []
        for qb in range(2):
            p = tile([P, 2, P, 2], F32, "p%d" % qb)
            l = tile([P, 1], F32, "l%d" % qb)
            nc.scalar.activation(p[:].rearrange("q u m r -> q (u m r)"), neg_c[:, qb, :], ACT.Exp,
                                 bias=neg_m[qb][:], scale=-1.0, accum_out=l[:])
            w = tile([P, 2, P, 2], BF16, "w%d" % qb)
            for u in range(2):
                nc.vector.tensor_tensor(w[:, u], p[:, u], vs_spread[:].rearrange("q (u m r) -> q u m r", u=2, r=2)[:, u],
                                        ALU.mult)
            weights.append(w)
            total.append(l)

        v_grouped = tile([P, DV * 4], BF16, "v_grouped", "neg_m1")
        nc.scalar.copy(v_grouped[:].bitcast(F32), v_turned[:].rearrange("p h e u -> p (h e u)"))
        v_codes = tile([P, DV], U32, "v_codes")
        v_plane = tile([P, DV], U8, "v_plane")
        nc.vector.quantize_mx(out=v_codes[:].bitcast(FP8X4), scales=v_plane[:], in_=v_grouped[:])

        for qb in range(2):
            w_turned = bank(2 + qb, [P, P, 2], "w_turned%d" % qb)
            words = weights[qb][:].rearrange("q u m r -> q u (m r)").bitcast(F32)
            for u in range(2):
                nc.tensor.transpose(w_turned[:, :, u], words[:, u, :], ident[:])
            w_grouped = tile([P, P * 4], BF16, "w_grouped%d" % qb)
            nc.scalar.copy(w_grouped[:].bitcast(F32), w_turned[:].rearrange("p q u -> p (q u)"))
            w_codes = tile([P, P], U32, "w_codes%d" % qb)
            w_plane = tile([P, P], U8, "w_plane%d" % qb)
            nc.vector.quantize_mx(out=w_codes[:].bitcast(FP8X4), scales=w_plane[:], in_=w_grouped[:])
            inverse = tile([P, 1], F32, "inverse%d" % qb)
            nc.vector.reciprocal(inverse[:], total[qb][:])
            y = tile([P, DV], F32, "y%d" % qb)
            width = DV // (qb + 1)
            for h in range(qb + 1):
                cols = slice(h * width, (h + 1) * width)
                sums = bank(4 + qb + h, [P, width], "sums%d_%d" % (qb, h))
                nc.tensor.matmul_mx(out=sums[:], lhsT=w_codes[:].bitcast(FP8X4), lhsT_scale=w_plane[:],
                                    rhs=v_codes[:, cols].bitcast(FP8X4), rhs_scale=v_plane[:, cols],
                                    start=True, stop=True)
                if h == 0:
                    nc.scalar.activation(y[:, cols], sums[:], ACT.Copy, scale=inverse[:])
                else:
                    nc.vector.tensor_scalar(out=y[:, cols], in0=sums[:], scalar1=inverse[:], scalar2=None, op0=ALU.mult)
            nc.sync.dma_start(out[0, qb * P:(qb + 1) * P, :], y[:])
